import numpy as np, ml_dtypes
CORES = [10,34,74,98]
N = 4
BF = ml_dtypes.bfloat16
def gentries(a):
    return np.ascontiguousarray(a.reshape(8, 16, -1).transpose(0, 2, 1)).reshape(8, -1)
def gtable(e):
    e = np.asarray(e); return np.ascontiguousarray(e.reshape(8, -1, 16).transpose(0, 2, 1)).reshape(128, -1).astype(np.int32)
W, K, NK, RO = 2048, 512, 3, 3
def sign(rng, *shape):
    return (2 * rng.integers(0, 2, shape) - 1).astype(np.float32)
def unit(rng, *shape):
    return rng.random(shape, dtype=np.float32)
def parts(rng, lo=-1, hi=0, gap=0.3):
    col = np.exp2(rng.integers(lo, hi + 1, (N, 8, 1, W))).astype(np.float32) * (unit(rng, N, 8, 1, W) >= gap)
    b = sign(rng, N, 8, 16, W) * (np.float32(0.75) + np.float32(0.5) * unit(rng, N, 8, 16, W)) * col
    w = sign(rng, N, 8, 16, W) * (np.float32(0.25) + np.float32(0.25) * unit(rng, N, 8, 16, W))
    rec = np.float32(0.25) + np.float32(0.75) * unit(rng, N, 8, 16, W)
    t = np.exp2(rng.integers(-8, -3, (N, 8, 1, 1))) * (0.7 + 0.6 * rng.random((N, 8, 16, 1)))
    p = np.argsort(rng.random((N, 8, NK + 2, W)), axis=-1)
    d = np.ascontiguousarray(np.argsort(rng.random((N, 8, W)), axis=-1)[..., :K])
    return b, w, rec, t, p, d
def pack(b, w, rec, t, p, d):
    return {"b0": b.reshape(N, 128, W).astype(BF), "w": w.reshape(N, 128, W).astype(BF), "rec": rec.reshape(N, 128, W).astype(BF), "th": t.reshape(N, 128, 1).astype(np.float32),
            "hop": np.ascontiguousarray(p[:, :, :NK].reshape(N, 8, NK * W)).astype(np.int32), "up": np.ascontiguousarray(p[:, :, NK]).astype(np.int32),
            "dn": np.ascontiguousarray(p[:, :, NK + 1]).astype(np.int32), "wk": np.stack([gtable(a) for a in d])}
def rest(rng, d):
    m = np.ones(W, bool); m[d] = False
    return rng.permutation(np.flatnonzero(m))
def goal(q, g, i):
    return (q, g) if i < NK else ((q + 1) % N, (g + 1) % 8) if i == NK else ((q - 1) % N, g)
def route(rng, d, y, shut, src=(), dst=()):
    y = y.copy(); f = y < 0; ok = ~shut; ok[y[~f]] = False
    y[f] = rng.permutation(np.flatnonzero(ok))[:np.count_nonzero(f)]
    d = np.concatenate([d, np.asarray(src, np.int64)]); y = np.concatenate([y, np.asarray(dst, np.int64)])
    p = np.zeros(W, np.int64); p[d] = y; a = np.ones(W, bool); a[d] = False; v = np.ones(W, bool); v[y] = False
    p[a] = rng.permutation(np.flatnonzero(v))
    return p
def odd(rng, *shape):
    return (2 * rng.integers(65, 127, shape) + 1).astype(np.float32)
def choose(ok, *v):
    i = np.argmax(ok, axis=0)[None]
    return [np.take_along_axis(a, i, 0)[0] for a in v]
def setup_inputs(rng):
    return pack(*parts(rng))
def setup_inputs_spread(rng):
    b, w, rec, t, p, d = parts(rng, -1, 1)
    w = sign(rng, N, 8, 16, W) * np.exp2(-4 + 3 * unit(rng, N, 8, 16, W)); rec = 0.0625 + 0.9375 * unit(rng, N, 8, 16, W)
    t = np.exp2(-11 + 9 * rng.random((N, 8, 16, 1)))
    return pack(b, w, rec, t, p, d)
def setup_inputs_ends(rng):
    M = K // 4; h = K // 2; s = sign(rng, 16)[:, None]; j = np.arange(M)
    size = rng.choice(np.array([64.0, 64.0, 2.0 ** -20, 0.0]), (N, 8, 1, W)).astype(np.float32)
    b = sign(rng, N, 8, 16, W) * size
    w = sign(rng, N, 8, 16, W) * rng.choice(np.array([0.5, 0.0625]), (N, 8, 1, W)).astype(np.float32)
    rec = np.where(unit(rng, N, 8, 16, W) < 0.5, np.float32(1), np.float32(0.0625))
    t = np.zeros((N, 8, 16, 1)); p = np.zeros((N, 8, NK + 2, W), np.int64); d = np.zeros((N, 8, K), np.int64); x = np.zeros((N, 8, 3, M), np.int64)
    for q in range(N):
        for g in range(8):
            d[q, g] = rng.permutation(np.concatenate([np.arange(h), W - h - g % 2 + np.arange(h)]))
            r = rest(rng, d[q, g]); r = r[np.argsort(r != W - 1, kind="stable")][:3 * M].reshape(3, M)
            x[q, g] = r if g % 4 == 3 else r[::-1]
            a = d[q, g, K - M:]; b[q, g][:, a] = 64 * s; w[q, g][:, a] = 0.5; rec[q, g][:, a] = 1
            b[q, g][:, x[q, g, 0]] = s * np.array([-64.0, 0.0, 64.0])[j % 3]
            b[q, g][:, x[q, g, 1]] = s * np.array([64.0, 0.0, 64.0])[j % 3]
            b[q, g][:, x[q, g, 2]] = -s * np.array([64.0, 0.0, 64.0, 63.75, 0.0, 64.0])[j % 6]
            xx = x[q, g].reshape(-1); w[q, g][:, xx] = 0.5; rec[q, g][:, xx] = 1
            n = (9, 16, 8, 10, 9, 12, 9, 16)[(g + q) % 8]
            t[q, g, :, 0] = np.where(rng.permutation(16) < n, 2.0 ** -20, 64.0)
    for q in range(N):
        for g in range(8):
            for i in range(NK + 2):
                xx = x[goal(q, g, i)]; y = np.full(K, -1); y[K - M:] = xx[0]; shut = np.zeros(W, bool); shut[xx.reshape(-1)] = True
                p[q, g, i] = route(rng, d[q, g], y, shut, x[q, g, :2].reshape(-1), xx[1:].reshape(-1))
    return pack(b, w, rec, t, p, d)
def setup_inputs_corners(rng):
    b, w, rec, t, p, d = parts(rng, 0, 0, 0.1); M = K // 2; L = K // 8; U = K // 16; e = np.float32(2.0 ** -9); e1 = np.float32(2.0 ** -8)
    x = np.zeros((N, 8, NK, M), np.int64); z = np.zeros((N, 8, 3, L), np.int64); xn = np.zeros((N, 8, 2, U), np.int64); shut = np.zeros((N, 8, W), bool)
    kind = (np.arange(N)[:, None] + np.arange(8)[None, :]) % 8; need = np.array([8, 9, 8, 9, 7, 10, 0, 16])[kind]
    late = (kind == 2) | (kind == 3); low = (need < 9)[:, :, None]
    tb = odd(rng, 64, N, 8, 16) * e1; tr = odd(rng, 64, N, 8, 16) * e1; tw = odd(rng, 64, N, 8, 16) * e; xw = odd(rng, 64, N, 8, 16) * e
    h = (tb * tr) * tw; top = h.astype(BF).astype(np.float32); h2 = top + (h - top).astype(BF).astype(np.float32)
    tb, tr, tw, xw = choose(np.where(low, h2 * xw > h * xw, h2 * xw < h * xw), tb, tr, tw, xw)
    gm = ((tb * tr) * tw) * xw
    yv = odd(rng, 256, N, 8, 16) * e1; yr = odd(rng, 256, N, 8, 16) * e1; zw = odd(rng, 256, N, 8, 16) * e; b2 = yv
    for k in range(NK): b2 = b2 + gm
    dl = b2 * yr; g2 = (xw * dl) * zw; g3 = dl * (xw * zw); g4 = (b2 * (yr * xw)) * zw
    yv, yr, zw, g2 = choose(np.where(low, (g3 > g2) & (g4 > g2), (g3 < g2) & (g4 < g2)), yv, yr, zw, g2)
    for q in range(N):
        for g in range(8):
            r = rest(rng, d[q, g]); xn[q, g] = r[:2 * U].reshape(2, U); r = r[2 * U:]
            for i in range(2):
                to = goal(q, g, NK + i); a = d[q, g, 8 + i * U:8 + (i + 1) * U]
                b[q, g][:, a] = tb[to][:, None] * sign(rng, 16, U); rec[q, g][:, a] = tr[to][:, None]; w[q, g][:, a] = tw[to][:, None] * sign(rng, 16, U)
            xx = xn[q, g].reshape(-1); b[q, g][:, xx] = 0; w[q, g][:, xx] = xw[q, g][:, None] * sign(rng, 16, 2 * U); shut[q, g, xx] = True
            n = int(need[q, g]); o = rng.permutation(16); gl = g2[q, g] if late[q, g] else gm[q, g]
            t[q, g, :, 0] = gl; t[q, g, o[:n], 0] = np.nextafter(gl[o[:n]], np.float32(0))
            if late[q, g]:
                z[q, g] = r[:3 * L].reshape(3, L); shut[q, g, r[:3 * L]] = True; sb = sign(rng, 16, L); sw = sign(rng, 16, L); sy = sign(rng, 16, L)
                a = d[q, g, K - L:]; b[q, g][:, a] = tb[q, g][:, None] * sb; rec[q, g][:, a] = tr[q, g][:, None]; w[q, g][:, a] = tw[q, g][:, None] * sw
                a = z[q, g, 0]; b[q, g][:, a] = -sb * sw * sy * yv[q, g][:, None]; rec[q, g][:, a] = yr[q, g][:, None]; w[q, g][:, a] = xw[q, g][:, None] * sy
                a = z[q, g, 1]; b[q, g][:, a] = 0; w[q, g][:, a] = zw[q, g][:, None] * sign(rng, 16, L)
                v = zw[q, g][:, None] * sign(rng, 16, L); ab = odd(rng, 16, L) * np.float32(2.0 ** -22) * sign(rng, 16, L); ar = odd(rng, 16, L) * e1; aw = odd(rng, 16, L) * e * sign(rng, 16, L)
                a = d[q, g, K - 2 * L:K - L]; b[q, g][:, a] = ab; rec[q, g][:, a] = ar; w[q, g][:, a] = aw
                a = z[q, g, 2]; w[q, g][:, a] = v; b[q, g][:, a] = (((ab * ar) * aw) * v).astype(BF).astype(np.float32)
                continue
            x[q, g] = r[:NK * M].reshape(NK, M); a = d[q, g, K - M:]
            b[q, g][:, a] = tb[q, g][:, None] * sign(rng, 16, M); rec[q, g][:, a] = tr[q, g][:, None]; w[q, g][:, a] = tw[q, g][:, None] * sign(rng, 16, M)
            xx = x[q, g].reshape(-1); v = np.repeat(xw[q, g][:, None], xx.size, axis=1); u = rng.integers(0, 5, xx.size); b[q, g][:, xx] = 0; shut[q, g, xx] = True
            if n > 0:
                j = np.flatnonzero(u == 1); v[o[rng.integers(0, n, j.size)], j] -= e
            if n < 16:
                j = np.flatnonzero(u == 2); v[o[rng.integers(n, 16, j.size)], j] += e
            j = np.flatnonzero(u == 3); b[q, g][rng.integers(0, 16, j.size), xx[j]] = np.float32(2.0 ** -20) * sign(rng, j.size)
            w[q, g][:, xx] = v * sign(rng, 16, xx.size)
    for q in range(N):
        for g in range(8):
            for i in range(NK + 2):
                y = np.full(K, -1); to = goal(q, g, i); src = np.zeros(0, np.int64); dst = src
                if i >= NK: y[8 + (i - NK) * U:8 + (i - NK + 1) * U] = xn[to][i - NK]
                elif late[q, g]:
                    y[K - L:] = z[q, g, 0]
                    if i == 0: y[K - 2 * L:K - L] = z[q, g, 2]
                    if i < 2: src = z[q, g, 0]; dst = z[q, g, 1 + i]
                else: y[K - M:] = x[q, g, i]
                if i == 0: y[:8] = d[q, g, :8]
                p[q, g, i] = route(rng, d[q, g], y, shut[to], src, dst)
    return pack(b, w, rec, t, p, d)
def setup_inputs_crowd(rng):
    b, w, rec, t, p, d = parts(rng, -1, -1); T = K // (2 * NK); M = K // 4
    x = np.zeros((N, 8, NK, M), np.int64); c = np.zeros((N, 8, T), np.int64); e = np.float32(2.0 ** -9)
    for q in range(N):
        for g in range(8):
            r = rest(rng, d[q, g]); c[q, g] = r[:T]; x[q, g] = r[T:T + NK * M].reshape(NK, M)
            m = d[q, g, :NK * T]; b[q, g][:, m] = sign(rng, 16, NK * T) * (0.75 + 0.5 * unit(rng, 16, NK * T))
            b[q, g][:, c[q, g]] = 2 * sign(rng, 16, T); rec[q, g][:, c[q, g]] = 0.5 + 0.25 * unit(rng, 16, T)
            j = np.arange(2, T, 3); b[q, g][rng.integers(0, 16, j.size), c[q, g, j]] = 0
            a = d[q, g, K - M:]; sb = sign(rng, 16, M); sw = sign(rng, 16, M)
            b[q, g][:, a] = sb * odd(rng, 16, M) * np.float32(2.0 ** -17); w[q, g][:, a] = sw * odd(rng, 16, M) * e; rec[q, g][:, a] = 0.5 + 0.5 * unit(rng, 16, M)
            o = np.argsort(rng.random((NK, 16, M)), axis=0)
            for k in range(NK):
                sx = sign(rng, 16, M); b[q, g][:, x[q, g, k]] = sx
                w[q, g][:, x[q, g, k]] = -sb * sw * sx * (200 + o[k]).astype(np.float32) * e
    for q in range(N):
        for g in range(8):
            for i in range(NK + 2):
                y = np.full(K, -1); shut = np.zeros(W, bool); z = goal(q, g, i); shut[x[z].reshape(-1)] = True; shut[c[z]] = True
                if i < NK:
                    y[i * T:(i + 1) * T] = np.where((np.arange(T) % 3 == 1) & (i == 0), -1, c[q, g]); y[K - M:] = x[q, g, i]
                p[q, g, i] = route(rng, d[q, g], y, shut)
    return pack(b, w, rec, t, p, d)
def setup_inputs_level(rng):
    b, w, rec, t, p, d = parts(rng)
    s = np.where(unit(rng, N, 8, 1, W) < 0.25, sign(rng, N, 8, 16, W), sign(rng, 1, 1, 16, 1) * sign(rng, N, 8, 1, W))
    b = s * np.exp2(rng.integers(-1, 1, (N, 8, 1, W))) * (unit(rng, N, 8, 1, W) >= 0.3)
    w = sign(rng, N, 8, 1, W) * np.exp2(rng.integers(-2, 0, (N, 8, 1, W))) + np.zeros((N, 8, 16, W))
    rec = np.exp2(rng.integers(-1, 1, (N, 8, 1, W))) + np.zeros((N, 8, 16, W))
    e = rng.integers(-6, -2, (N, 8, 1, 1)).astype(np.float64); n = rng.integers(8, 10, (N, 8, 1, 1))
    t = np.where(np.argsort(rng.random((N, 8, 16, 1)), axis=2) < n, np.exp2(e - 1), np.exp2(e))
    return pack(b, w, rec, t, p, d)
def check_ranges(d):
    bad = []
    for k in ("hop", "up", "dn", "wk"):
        if np.min(d[k]) < 0 or np.max(d[k]) > W - 1: bad.append("range of " + k)
    for k in ("hop", "up", "dn"):
        if np.any(np.sort(np.asarray(d[k]).reshape(N, 8, -1, W), axis=-1) != np.arange(W)): bad.append(k + " is no permutation")
    e = np.sort(np.stack([gentries(np.asarray(a)) for a in d["wk"]]), axis=-1)
    if np.any(e[..., 1:] == e[..., :-1]): bad.append("wk names a place twice in a group")
    a = np.abs(np.asarray(d["b0"]).astype(np.float32))
    if not np.all((a == 0) | ((a >= 2.0 ** -20) & (a <= 64))): bad.append("range of b0")
    a = np.abs(np.asarray(d["w"]).astype(np.float32))
    if not np.all((a >= 0.0625) & (a <= 0.5)): bad.append("range of w")
    a = np.asarray(d["rec"]).astype(np.float32)
    if not np.all((a >= 0.0625) & (a <= 1)): bad.append("range of rec")
    a = np.asarray(d["th"]).astype(np.float32)
    if not np.all((a >= 2.0 ** -20) & (a <= 64)): bad.append("range of th")
    return bad
def pick(a, ix):
    return np.take_along_axis(a, ix[:, :, None, :], 3)
def place(a, ix, v):
    np.put_along_axis(a, ix[:, :, None, :], v, 3)
def arrive(b, wf, t, x, h):
    g = h * pick(wf, x); o = pick(b, x)
    new = np.all(o == 0, axis=2, keepdims=True); few = np.sum(np.abs(g) > t, axis=2, keepdims=True) < 9
    place(b, x, np.where(new & few, o, o + g))
def reference(b0, w, rec, th, hop, up, dn, wk):
    b = b0.astype(np.float32).reshape(N, 8, 16, W).copy(); wf = w.astype(np.float32).reshape(N, 8, 16, W); rf = rec.astype(np.float32).reshape(N, 8, 16, W)
    t = th.astype(np.float32).reshape(N, 8, 16, 1); hp = hop.astype(np.int64).reshape(N, 8, NK, W); ul = up.astype(np.int64); dl = dn.astype(np.int64)
    d = np.stack([gentries(a) for a in wk]).astype(np.int64); c = np.zeros((N, 8, 16, W), np.float32)
    for s in range(RO):
        delta = -(pick(b, d) * pick(rf, d))
        place(c, d, pick(c, d) + delta); place(b, d, np.float32(0))
        h = pick(wf, d) * delta
        xs = [np.take_along_axis(hp[:, :, k], d, 2) for k in range(NK)]
        for x in xs: arrive(b, wf, t, x, h)
        x = np.take_along_axis(ul, d, 2); arrive(b, wf, t, np.roll(x, (1, 1), (0, 1)), np.roll(h, (1, 1), (0, 1)))
        x = np.take_along_axis(dl, d, 2); arrive(b, wf, t, np.roll(x, -1, 0), np.roll(h, -1, 0))
        if s == RO - 1: break
        m = np.stack([np.abs(pick(b, x)) for x in xs])
        votes = np.sum(m == np.max(m, axis=0), axis=3)
        ch = np.argmax(votes, axis=0)
        to = np.take_along_axis(np.stack(xs), ch[None], 0)[0]
        held = np.zeros((N, 8, W), bool); np.put_along_axis(held, d, True, 2)
        first = np.full((N, 8, W), NK)
        for k in range(NK - 1, -1, -1):
            qq, gg, jj = np.nonzero(ch == k); first[qq, gg, to[qq, gg, jj]] = k
        go = ~np.take_along_axis(held, to, 2) & (np.take_along_axis(first, to, 2) == ch)
        d = np.where(go, to, d)
    return {"yb": b.reshape(N, 128, W), "yc": c.reshape(N, 128, W)}

def check_inputs(d):
    bad = list(check_ranges(d))
    if not bad:
        for name, y in reference(**d).items():
            for q in range(N):
                v = np.abs(np.asarray(y[q], np.float64)); s = np.sqrt(np.mean(v * v))
                if v.max() > 9 * s or s < 2.0 ** -3: bad.append('%s of rank %d is uneven or too small' % (name, q))
    return bad

@@ -1,0 +1,408 @@
+from concourse.mybir import AluOpType, ActivationFunctionType
+
+W, K, RO = 2048, 512, 3
+F32, BF, I32, U16 = "float32", "bfloat16", "int32", "uint16"
+MSG = K + 64
+ROW0, ROWS = 0, 3
+THR = 8.5 * 2.0 ** -20
+SELW = 8192.0
+
+SCRATCH = {
+    "bb": ("sbuf", [128, W], F32), "cc": ("sbuf", [128, W], F32), "held": ("sbuf", [128, W], F32),
+    "tb": ("sbuf", [128, W], I32), "first": ("sbuf", [128, 3 * W], BF),
+    "b0s": ("sbuf", [128, W], BF), "ws": ("sbuf", [128, W], BF), "recs": ("sbuf", [128, W], BF),
+    "ths": ("sbuf", [128, 8], F32), "nth": ("sbuf", [128, 8], F32),
+    "zin": ("sbuf", [128, K], F32), "sh0": ("sbuf", [128, K], F32), "sh1": ("sbuf", [128, K], F32),
+    "sf0": ("sbuf", [128, K], BF), "sf1": ("sbuf", [128, K], BF),
+    "ones": ("sbuf", [128, 160], F32), "jj": ("sbuf", [128, 160], F32),
+    "pe": ("sbuf", [128, 160], F32), "po": ("sbuf", [128, 160], F32),
+    "bd0": ("sbuf", [128, 128], BF), "bd1": ("sbuf", [128, 128], BF), "bda": ("sbuf", [128, 128], BF),
+    "bdb": ("sbuf", [128, 128], BF), "sel": ("sbuf", [128, 144], BF),
+    "d0": ("sbuf", [128, 32], I32), "d1": ("sbuf", [128, 32], I32), "d2": ("sbuf", [128, 32], I32),
+    "d16": ("sbuf", [128, 32], U16), "xl": ("sbuf", [128, 96], U16), "xu": ("sbuf", [128, 32], U16),
+    "xd": ("sbuf", [128, 32], U16), "lw16": ("sbuf", [128, 64], U16),
+    "nb": ("sbuf", [128, K], F32), "dl": ("sbuf", [128, K], F32), "cd": ("sbuf", [128, K], F32),
+    "tg": ("sbuf", [128, K], F32), "tr": ("sbuf", [128, 16, 2, 16], F32),
+    "g0": ("sbuf", [128, K], F32), "g1": ("sbuf", [128, K], F32), "g2": ("sbuf", [128, K], F32),
+    "sm": ("sbuf", [128, K], F32), "mk": ("sbuf", [128, K], F32), "mt": ("sbuf", [128, K // 2], F32),
+    "ag": ("sbuf", [128, K], F32), "rl": ("sbuf", [128, K], F32), "ov": ("sbuf", [128, K], BF),
+    "ab": ("sbuf", [128, K], BF),
+    "mm": ("sbuf", [128, 3, K], F32), "vv": ("sbuf", [128, 3, K], BF),
+    "xk": ("sbuf", [128, 3, 32], F32), "key": ("sbuf", [128, 3, 32], I32), "k01": ("sbuf", [128, 32], I32),
+    "kk": ("sbuf", [128, 32], I32), "lw": ("sbuf", [128, 64], I32), "rr": ("sbuf", [128, 32], I32),
+    "thr": ("sbuf", [128, 32], F32), "dif": ("sbuf", [128, 32], I32), "tt": ("sbuf", [128, 32], F32),
+    "go": ("sbuf", [128, 32], I32), "dd": ("sbuf", [128, 32], I32),
+    "hg": ("sbuf", [128, K], BF), "lk": ("sbuf", [128, 2, K], BF),
+    "pa0": ("psum", [128, K], F32), "pb0": ("psum", [128, K], F32),
+    "pa1": ("psum", [128, K], F32), "pb1": ("psum", [128, K], F32),
+    "pl": ("psum", [128, 32, 16], F32), "pm": ("psum", [128, K], F32),
+    "pv": ("psum", [128, 16, 32], F32), "pk": ("psum", [128, 16, 32], F32),
+}
+for _s in range(RO):
+    for _n in ("snd", "lu", "lr", "ld"):
+        SCRATCH["%s%d" % (_n, _s)] = ("sbuf", [128, MSG], F32)
+PSUM = ("pa0", "pb0", "pa1", "pb1", "pl", "pm", "pv", "pk")
+
+SEMAPHORES = ["cV", "cA", "cP", "cG", "l_wk", "l_th", "l_b0", "l_rec", "l_w", "l_tb", "sent", "o_c", "o_b"]
+for _s in range(RO):
+    SEMAPHORES += ["au%d" % _s, "ad%d" % _s, "rot%d" % _s]
+
+
+def new_plan():
+    return {"ops": [], "writer": {}, "readers": {}, "known": {q: ({}, set()) for q in "VAPGS"}, "n": {q: 0 for q in "VAPG"}}
+
+
+def add(plan, q, fn, reads=(), writes=(), dma=None):
+    op = {"q": q, "fn": fn, "dma": dma, "waits": [], "need": False, "id": len(plan["ops"])}
+    if dma is None:
+        op["idx"] = plan["n"][q]
+        plan["n"][q] += 1
+    deps = []
+    for k in reads:
+        if k in plan["writer"]:
+            deps.append(plan["writer"][k])
+        if k in PSUM:
+            deps += [r for r in plan["readers"].get(k, []) if r["q"] != q]
+    for k in writes:
+        if k in plan["writer"]:
+            deps.append(plan["writer"][k])
+        deps += plan["readers"].get(k, [])
+    if q is not None:
+        cnt, done = plan["known"][q]
+        deps.sort(key=lambda d: -d["id"])
+        for d in deps:
+            if d["dma"] is None:
+                if d["q"] == "P" and q == "P":
+                    continue
+                if cnt.get(d["q"], -1) >= d["idx"]:
+                    continue
+                cnt[d["q"]] = d["idx"]
+            else:
+                if d["id"] in done:
+                    continue
+                done.add(d["id"])
+            d["need"] = True
+            op["waits"].append(d)
+            for e, v in d["clock"][0].items():
+                if cnt.get(e, -1) < v:
+                    cnt[e] = v
+            done.update(d["clock"][1])
+        op["clock"] = (dict(cnt), set(done))
+    else:
+        op["clock"] = ({}, set())
+    for k in reads:
+        plan["readers"].setdefault(k, []).append(op)
+    for k in writes:
+        plan["writer"][k] = op
+        plan["readers"][k] = []
+    plan["ops"].append(op)
+    return op
+
+
+def emit(plan, g, T):
+    qs = {"V": g.vector, "A": g.scalar, "P": g.tensor, "G": g, "S": g.sync}
+    cnt = {q: 0 for q in "VAPG"}
+    for op in plan["ops"]:
+        if op["dma"] is None and op["need"]:
+            cnt[op["q"]] += 1
+            op["val"] = cnt[op["q"]]
+    for op in plan["ops"]:
+        if op["q"] is None:
+            continue
+        for d in op["waits"]:
+            if d["dma"] is None:
+                qs[op["q"]].wait_ge(T.sem["c" + d["q"]], d["val"])
+            else:
+                qs[op["q"]].wait_ge(T.sem[d["dma"][0]], d["dma"][1])
+        ins = op["fn"]()
+        if op["dma"] is None and op["need"]:
+            ins.then_inc(T.sem["c" + op["q"]], 1)
+
+
+def rank_program(g, core, T, topo):
+    rank = T.rank_of(core)
+    if rank is None:
+        return
+    n = len(T.cores)
+    A, Fn = AluOpType, ActivationFunctionType
+    V, S, P, Y = g.vector, g.scalar, g.tensor, g.sync
+    plan = new_plan()
+    C2 = ["cL", "cR"]
+    H = K // 2
+
+    def op(q, fn, reads=(), writes=(), dma=None):
+        return add(plan, q, fn, reads, writes, dma)
+
+    def win(name, lst, a=0, b=W):
+        return T[name][:, a:b].indirect(lst)
+
+    def load(q, eng, dst, src, sem, key):
+        op(q, lambda: eng.dma_start(dst, src).then_inc(T.sem[sem], 16), [], [key], (sem, 16))
+
+    load("S", Y, T.d0[:], T.wk[:], "l_wk", "d0")
+    load("S", Y, T.b0s[:], T.b0[:], "l_b0", "b0s")
+    load("A", S, T.recs[:], T.rec[:], "l_rec", "recs")
+    load("A", S, T.ws[:], T.w[:], "l_w", "ws")
+    op("V", lambda: V.memset(T.bd0[:], 2.0 ** 46), [], ["bd0"])
+    op("V", lambda: V.memset(T.ones[:], 1.0), [], ["ones"])
+    op("V", lambda: V.memset(T.zin[:], -128.0), [], ["zin"])
+    op("V", lambda: V.memset(T.tb[:], 0), [], ["tb"])
+    op("V", lambda: V.memset(T.sel[:], 0.0), [], ["sel"])
+
+    def tables():
+        for t in range(5):
+            src = T.hop[:, t * W:(t + 1) * W] if t < 3 else (T.up[:] if t == 3 else T.dn[:])
+            Y.dma_start(T.tb[ROW0 + ROWS * t::16, :], src).then_inc(T.sem.l_tb, 16)
+    op("S", tables, [], ["tb"], ("l_tb", 80))
+
+    op("G", lambda: g.affine_select(T.jj[:], T.ones[:], [[1, 160]], A.is_equal, 0.0, -16, -1), ["ones"], ["jj"])
+    op("G", lambda: g.affine_select(T.bd1[:], T.bd0[:], [[-16, 8], [0, 16]], A.is_ge, 0.0, 0, 1), ["bd0"], ["bd1"])
+    op("G", lambda: g.affine_select(T.pe[:], T.jj[:], [[0, 5], [1, 2], [0, 16]], A.is_gt, 0.0, 0, 0), ["jj"], ["pe"])
+    op("G", lambda: g.affine_select(T.po[:], T.jj[:], [[0, 5], [1, 2], [0, 16]], A.is_equal, 0.0, 0, 0), ["jj"], ["po"])
+    op("G", lambda: g.affine_select(T.bda[:], T.bd1[:], [[16, 8], [0, 16]], A.is_ge, 0.0, 15, -1), ["bd1"], ["bda"])
+    op("G", lambda: g.dma_start(T.ths[:, 0:1], T.th[:], allow_slow_non_contiguous=True).then_inc(T.sem.l_th, 16),
+       [], ["ths"], ("l_th", 16))
+
+    def gfill(ap, cols, val, key):
+        op("G", lambda: g.iota(ap, [[0, cols]], val, 0, allow_small_or_imprecise_dtypes=True), [], [key])
+    gfill(T.cc[:, W // 2:W], W // 2, 0, "cR")
+    for j in range(2):
+        op("A", lambda j=j: S.activation(T.cc[:, j * K:(j + 1) * K], T.zin[:], Fn.Silu), ["zin"], ["cL"])
+    op("A", lambda: S.activation(T.bb[:], T.b0s[:], Fn.Copy), ["b0s"], ["bb"])
+    op("V", lambda: V.tensor_copy(T.d16[:], T.d0[:]), ["d0"], ["d16"])
+
+    def zero_b():
+        op("A", lambda: S.activation(win("bb", T.d16[:]), T.zin[:], Fn.Silu), ["zin", "d16"], ["bb"])
+
+    def table_gather():
+        op("V", lambda: V.tensor_copy(T.tg[:], win("tb", T.d16[:])), ["tb", "d16"], ["tg"])
+        op("V", lambda: V.transpose(T.tr[:], T.tg[:]), ["tg"], ["tr"])
+
+        def sort_groups():
+            last = None
+            for cp in range(2):
+                m = T.pe if cp == 0 else T.po
+                for gp in range(2):
+                    a = 16 - 16 * (gp - cp)
+                    last = P.matmul(T.pl[:, cp::2, 0:5], m[:, a:a + 128],
+                                    T.tr[:, :, gp, ROW0:ROW0 + 4 * ROWS + 1:ROWS], gp == 0, gp == 1)
+            return last
+        op("P", sort_groups, ["tr", "pe", "po"], ["pl"])
+
+    def hop_list(k):
+        op("V", lambda: V.tensor_copy(T.xl[:, 32 * k:32 * k + 32], T.pl[:, :, k]), ["pl"], ["x%d" % k])
+
+    def lists_and_send(s):
+        snd = T["snd%d" % s]
+        hop_list(0)
+        op("V", lambda: V.tensor_copy(snd[:, K:MSG], T.pl[:, :, 3:5]), ["pl"], ["sl%d" % s])
+        for dst, land, sem in ((T.cores[(rank + 1) % n], "lu", "au"), (T.cores[(rank - 1) % n], "ld", "ad")):
+            def send(dst=dst, land=land, sem=sem):
+                rid, pid, _e = topo.addr(dst)
+                g.remote_dma(T["%s%d" % (land, s)][:], snd[:], T.sem["%s%d" % (sem, s)], T.sem.sent, pid, rid,
+                             topo.mask(core, dst))
+            op("G", send, ["h%d" % s, "sl%d" % s], [], ("sent", 0))
+        op(None, None, [], ["lu%d" % s], ("au%d" % s, len(topo.engines(T.cores[(rank - 1) % n], core))))
+        op(None, None, [], ["ld%d" % s], ("ad%d" % s, len(topo.engines(T.cores[(rank + 1) % n], core))))
+
+        def turn():
+            Y.dma_start(T["lr%d" % s][16:128, :], T["lu%d" % s][0:112, :]).then_inc(T.sem["rot%d" % s], 16)
+            Y.dma_start(T["lr%d" % s][0:16, :], T["lu%d" % s][112:128, :]).then_inc(T.sem["rot%d" % s], 16)
+        op("S", turn, ["lu%d" % s], ["lr%d" % s], ("rot%d" % s, 32))
+
+    def c_scatter(s, a, b):
+        lst = T.d16[:, a // 16:b // 16]
+        if s == 0:
+            op("V", lambda: V.tensor_copy(win("cc", lst), T.dl[:, a:b]), ["dl", "d16"], C2)
+        else:
+            op("V", lambda: V.tensor_tensor(win("cc", lst), T.cd[:, a:b], T.dl[:, a:b], A.add), ["dl", "cd%d" % a, "d16"], C2)
+
+    def c_gather(a, b):
+        op("A", lambda: S.activation(T.cd[:, a:b], win("cc", T.d16[:, a // 16:b // 16]), Fn.Copy), C2 + ["d16"], ["cd%d" % a])
+
+    def arrival(s, k):
+        if k < 3:
+            return T.xl[:, 32 * k:32 * k + 32], "x%d" % k, T["snd%d" % s][:, 0:K], "h%d" % s
+        if k == 3:
+            return T.xu[:], "xu", T["lr%d" % s][:, 0:K], "lr%d" % s
+        return T.xd[:], "xd", T["ld%d" % s][:, 0:K], "ld%d" % s
+
+    def make_g(s, k):
+        lst, lk, h, hk = arrival(s, k)
+        if k == 3:
+            op("V", lambda: V.tensor_copy(T.xu[:], T["lr%d" % s][:, K:MSG:2]), [hk], ["xu"])
+        if k == 4:
+            op("V", lambda: V.tensor_copy(T.xd[:], T["ld%d" % s][:, K + 1:MSG:2]), [hk], ["xd"])
+        gb = "g%d" % (k % 3)
+        op("V", lambda: V.tensor_tensor(T[gb][:], win("ws", lst), h, A.mult), ["ws", lk, hk], [gb])
+
+    def banks(s, k):
+        par = (5 * s + k) % 2
+        return "pa%d" % par, "pb%d" % par
+
+    def over(s, k, opens=True):
+        gb = "g%d" % (k % 3)
+        pa, pb = banks(s, k)
+        op("A", lambda: S.activation(T.ag[:], T[gb][:], Fn.Abs), [gb], ["ag"])
+        op("A", lambda: S.activation(T.rl[:], T.ag[:], Fn.Relu, bias=T.nth[:, 0:1]), ["ag", "nth"], ["rl"])
+        op("A", lambda: S.activation(T.ov[:], T.rl[:], Fn.Sign), ["rl"], ["ov"])
+
+        def count():
+            P.matmul(T[pa][:, 0:H], T.bdb[:], T.ov[:, 0:H], opens, not opens)
+            return P.matmul(T[pb][:, 0:H], T.bdb[:], T.ov[:, H:K], opens, not opens)
+        op("P", count, ["ov", "bdb"], [pa, pb])
+
+    def empty(s, k, opens=False):
+        lst, lk, _h, _hk = arrival(s, k)
+        pa, pb = banks(s, k)
+        op("A", lambda: S.activation(T.ab[:], win("bb", lst), Fn.Abs, scale=2.0 ** 64), ["bb", lk], ["ab"])
+        op("P", lambda: P.matmul(T[pa][:, 0:H], T.bda[:], T.ab[:, 0:H], opens, not opens), ["ab", "bda"], [pa])
+        op("P", lambda: P.matmul(T[pb][:, 0:H], T.bda[:], T.ab[:, H:K], opens, not opens), ["ab", "bda"], [pb])
+
+    def make_sum(s, k):
+        lst, lk, _h, _hk = arrival(s, k)
+        gb = "g%d" % (k % 3)
+        op("V", lambda: V.tensor_tensor(T.sm[:], win("bb", lst), T[gb][:], A.add), ["bb", lk, gb], ["sm"])
+
+    def mask_b(s, k):
+        pb = banks(s, k)[1]
+        op("A", lambda: S.activation(T.mt[:], T[pb][:, 0:H], Fn.Relu, bias=-THR), [pb], ["mt"])
+        op("A", lambda: S.activation(T.mk[:, H:K], T.mt[:], Fn.Sign), ["mt"], ["mkB"])
+
+    def put(s, k, both):
+        lst, lk, _h, _hk = arrival(s, k)
+        pa, pb = banks(s, k)
+        op("V", lambda: V.tensor_scalar(T.mk[:, 0:H], T[pa][:, 0:H], THR, None, A.is_gt), [pa], ["mkA"])
+        if both:
+            op("V", lambda: V.tensor_scalar(T.mk[:, H:K], T[pb][:, 0:H], THR, None, A.is_gt), [pb], ["mkB"])
+        op("V", lambda: V.tensor_tensor(win("bb", lst), T.sm[:], T.mk[:], A.mult), ["sm", "mkA", "mkB", lk], ["bb"])
+
+    def keys():
+        for k in range(3):
+            op("A", lambda k=k: S.activation(T.xk[:, k, :], T.pl[:, :, k], Fn.Identity, bias=float((2 - k) * W)),
+               ["pl"], ["xk"])
+
+    def election(s):
+        dn_, do_ = "d%d" % (s + 1), "d%d" % s
+        for hf in range(2):
+            a, b = hf * H, (hf + 1) * H
+            for k in range(3):
+                lst = T.xl[:, 32 * k + 16 * hf:32 * k + 16 * hf + 16]
+                op("A", lambda k=k, lst=lst, a=a, b=b: S.activation(T.mm[:, k, a:b], win("bb", lst), Fn.Abs),
+                   ["bb", "x%d" % k], ["m%d%d" % (k, hf)])
+        op("A", lambda: S.activation(win("held", T.d16[:]), T["sh%d" % s][:], Fn.Silu), ["sh%d" % s, "d16"], ["held"])
+        for hf in range(2):
+            a, b = hf * H, (hf + 1) * H
+            op("V", lambda a=a, b=b: V.tensor_tensor(T.pm[:, a:b], T.mm[:, 0, a:b], T.mm[:, 1, a:b], A.max),
+               ["m0%d" % hf, "m1%d" % hf], ["pm%d" % hf])
+            op("V", lambda a=a, b=b: V.tensor_tensor(T.pm[:, a:b], T.pm[:, a:b], T.mm[:, 2, a:b], A.max),
+               ["pm%d" % hf, "m2%d" % hf], ["pm%d" % hf])
+            for k in range(3):
+                op("V", lambda k=k, a=a, b=b: V.tensor_tensor(T.vv[:, k, a:b], T.pm[:, a:b], T.mm[:, k, a:b], A.is_equal),
+                   ["pm%d" % hf, "m%d%d" % (k, hf)], ["v%d%d" % (k, hf)])
+
+            def votes(hf=hf, a=a, b=b):
+                last = None
+                for i in range(16):
+                    last = P.matmul(T.pv[:, 0:3, 16 * hf:16 * hf + 16], T.sel[:, 15 - i:143 - i], T.vv[:, :, a + i:b:16],
+                                    i == 0, i == 15)
+                return last
+            op("P", votes, ["sel", "v0%d" % hf, "v1%d" % hf, "v2%d" % hf], ["pv"])
+        op("V", lambda: V.tensor_tensor(T.key[:], T.pv[:, 0:3, :], T.xk[:], A.add), ["pv", "xk"], ["key"])
+        op("V", lambda: V.tensor_tensor(T.k01[:], T.key[:, 0, :], T.key[:, 1, :], A.max), ["key"], ["k01"])
+        op("V", lambda: V.tensor_tensor(T.kk[:], T.k01[:], T.key[:, 2, :], A.max), ["key", "k01"], ["kk"])
+        op("V", lambda: V.tensor_scalar(T.lw[:, 0:32], T.kk[:], 4 * W - 1, None, A.bitwise_and), ["kk"], ["lwL"])
+        op("V", lambda: V.tensor_scalar(T.lw[:, 32:64], T.kk[:], W - 1, None, A.bitwise_and), ["kk"], ["lwW"])
+        op("V", lambda: V.tensor_copy(T.lw16[:], T.lw[:]), ["lwL", "lwW"], ["lw16"])
+        wish = T.lw16[:, 32:64]
+        op("V", lambda: V.tensor_copy(win("first", T.lw16[:, 0:32], 0, 3 * W), T["sf%d" % s][:]),
+           ["lw16", "sf%d" % s], ["first"])
+        op("A", lambda: S.activation(T.hg[:], win("held", wish), Fn.Copy, scale=0.125), ["held", "lw16"], ["hg"])
+        op("A", lambda: S.activation(T.lk[:, 0, :], win("first", wish, 2 * W, 3 * W), Fn.Copy, scale=2.0),
+           ["first", "lw16"], ["lkA"])
+        op("V", lambda: V.tensor_tensor(T.lk[:, 1, :], win("first", wish, W, 2 * W), T.hg[:], A.add),
+           ["first", "lw16", "hg"], ["lkB"])
+
+        def look():
+            last = None
+            for i in range(16):
+                last = P.matmul(T.pk[:, 0:2, :], T.sel[:, 15 - i:143 - i], T.lk[:, :, i::16], i == 0, i == 15)
+            return last
+        op("P", look, ["sel", "lkA", "lkB"], ["pk"])
+        u = 16.0 * SELW
+        al, be = ((1.5 * u / W, 0.25 * u), (24.0 * u / W, 8.0 * u))[s]
+        op("V", lambda: V.tensor_tensor(T.rr[:], T.lw[:, 0:32], T.lw[:, 32:64], A.subtract), ["lwL", "lwW"], ["rr"])
+        op("V", lambda: V.tensor_tensor(T.dif[:], T.lw[:, 32:64], T[do_][:], A.subtract), ["lwW", do_], ["dif"])
+        op("V", lambda: V.tensor_scalar(T.thr[:], T.rr[:], al, be, A.mult, A.add), ["rr"], ["thr"])
+        op("V", lambda: V.tensor_tensor(T.tt[:], T.thr[:], T.pk[:, 0, :], A.subtract), ["thr", "pk"], ["tt"])
+        op("V", lambda: V.tensor_tensor(T.go[:], T.pk[:, 1, :], T.tt[:], A.is_lt), ["tt", "pk"], ["go"])
+        op("V", lambda: V.tensor_tensor(T.dd[:], T.go[:], T.dif[:], A.mult), ["go", "dif"], ["dd"])
+        op("V", lambda: V.tensor_tensor(T[dn_][:], T.dd[:], T[do_][:], A.add), ["dd", do_], [dn_])
+        op("V", lambda: V.tensor_copy(T.d16[:], T[dn_][:]), [dn_], ["d16"])
+
+    for s in range(RO):
+        h = T["snd%d" % s][:, 0:K]
+        hk = "h%d" % s
+        if s == 0:
+            zero_b()
+            op("A", lambda: S.activation(T.nth[:, 0:1], T.ths[:, 0:1], Fn.Copy, scale=-1.0), ["ths"], ["nth"])
+            op("A", lambda: S.activation(T.bdb[:], T.bda[:], Fn.Copy, scale=2.0 ** -66), ["bda"], ["bdb"])
+            op("A", lambda: S.activation(T.sel[:, 15:128:16], T.bda[:, 15:128:16], Fn.Copy, scale=SELW * 2.0 ** -46),
+               ["bda", "sel"], ["sel"])
+            op("V", lambda: V.tensor_scalar(T.nb[:], win("b0s", T.d16[:]), -1.0, None, A.mult), ["b0s", "d16"], ["nb"])
+            op("V", lambda: V.tensor_tensor(T.dl[:], win("recs", T.d16[:]), T.nb[:], A.mult), ["recs", "d16", "nb"], ["dl"])
+            table_gather()
+        else:
+            op("A", lambda: S.activation(T.nb[:], win("bb", T.d16[:]), Fn.Copy, scale=-1.0), ["bb", "d16"], ["nb"])
+            zero_b()
+            c_gather(0, H)
+            table_gather()
+            op("V", lambda: V.tensor_tensor(T.dl[:], win("recs", T.d16[:]), T.nb[:], A.mult), ["recs", "d16", "nb"], ["dl"])
+        op("V", lambda h=h: V.tensor_tensor(h, win("ws", T.d16[:]), T.dl[:], A.mult), ["ws", "d16", "dl"], [hk])
+        lists_and_send(s)
+        if s == 0:
+            gfill(T.held[:], W, 0, "held")
+            gfill(T.sh0[:], K, 32, "sh0")
+            gfill(T.sf0[:], K, 1, "sf0")
+            gfill(T.first[:, W:3 * W], 2 * W, 0, "first")
+            gfill(T.sh1[:], K, 512, "sh1")
+            gfill(T.sf1[:], K, 16, "sf1")
+        last = s == RO - 1
+        empty(s, 0, True)
+        make_g(s, 0)
+        over(s, 0, False)
+        hop_list(1)
+        hop_list(2)
+        make_g(s, 1)
+        make_sum(s, 0)
+        if last:
+            c_scatter(s, 0, H)
+        for k in range(5):
+            if k > 0:
+                empty(s, k)
+                make_sum(s, k)
+                if k < 4:
+                    make_g(s, k + 1)
+            if k < 4:
+                mask_b(s, k)
+            elif last:
+                c_scatter(s, H, K)
+                op("S", lambda: Y.dma_start(T.yc[:], T.cc[:]).then_inc(T.sem.o_c, 16), C2, ["yc"], ("o_c", 16))
+            else:
+                c_scatter(s, 0, H)
+            put(s, k, k == 4)
+            if k < 4:
+                over(s, k + 1)
+            if k == 0 and not last:
+                keys()
+            if k == 1 and s > 0:
+                c_gather(H, K)
+        if not last:
+            c_scatter(s, H, K)
+            election(s)
+
+    op("S", lambda: Y.dma_start(T.yb[:], T.bb[:]).then_inc(T.sem.o_b, 16), ["bb"], ["yb"], ("o_b", 16))
+    emit(plan, g, T)
+    Y.wait_ge(T.sem.o_c, 16)
+    Y.wait_ge(T.sem.o_b, 16)
+    g.wait_ge(T.sem.sent, RO * (len(topo.engines(core, T.cores[(rank + 1) % n])) + len(topo.engines(core, T.cores[(rank - 1) % n]))))

@@ -1,8 +1,10 @@
 from concourse.mybir import AluOpType, ActivationFunctionType
 
 W, K, RO = 2048, 512, 3
-F32, BF, I32, U16 = "float32", "bfloat16", "int32", "uint16"
+F32, BF, F16, I32, U16 = "float32", "bfloat16", "float16", "int32", "uint16"
 MSG = K + 64
+MA = 384
+CUTS = [[0, 0, 192, 352, 512], [0, 128, 256, 384, 512], [0, 256, 512]]
 ROW0, ROWS = 0, 3
 THR = 8.5 * 2.0 ** -20
 SELW = 8192.0
@@ -15,16 +17,16 @@ SCRATCH = {
     "zin": ("sbuf", [128, K], F32), "sh0": ("sbuf", [128, K], F32), "sh1": ("sbuf", [128, K], F32),
     "sf0": ("sbuf", [128, K], BF), "sf1": ("sbuf", [128, K], BF),
     "ones": ("sbuf", [128, 160], F32), "jj": ("sbuf", [128, 160], F32),
-    "pe": ("sbuf", [128, 160], F32), "po": ("sbuf", [128, 160], F32),
+    "pe": ("sbuf", [128, 160], F16), "po": ("sbuf", [128, 160], F16),
     "bd0": ("sbuf", [128, 128], BF), "bd1": ("sbuf", [128, 128], BF), "bda": ("sbuf", [128, 128], BF),
     "bdb": ("sbuf", [128, 128], BF), "sel": ("sbuf", [128, 144], BF),
     "d0": ("sbuf", [128, 32], I32), "d1": ("sbuf", [128, 32], I32), "d2": ("sbuf", [128, 32], I32),
     "d16": ("sbuf", [128, 32], U16), "xl": ("sbuf", [128, 96], U16), "xu": ("sbuf", [128, 32], U16),
     "xd": ("sbuf", [128, 32], U16), "lw16": ("sbuf", [128, 64], U16),
     "nb": ("sbuf", [128, K], F32), "dl": ("sbuf", [128, K], F32), "cd": ("sbuf", [128, K], F32),
-    "tg": ("sbuf", [128, K], F32), "tr": ("sbuf", [128, 16, 2, 16], F32),
+    "tg": ("sbuf", [128, K], F16), "tr": ("sbuf", [128, 16, 2, 16], F16),
     "g0": ("sbuf", [128, K], F32), "g1": ("sbuf", [128, K], F32), "g2": ("sbuf", [128, K], F32),
-    "sm": ("sbuf", [128, K], F32), "mk": ("sbuf", [128, K], F32), "mt": ("sbuf", [128, K // 2], F32),
+    "sm": ("sbuf", [128, K], F32), "mk": ("sbuf", [128, K], F32), "mt": ("sbuf", [128, K - MA], F32),
     "ag": ("sbuf", [128, K], F32), "rl": ("sbuf", [128, K], F32), "ov": ("sbuf", [128, K], BF),
     "ab": ("sbuf", [128, K], BF),
     "mm": ("sbuf", [128, 3, K], F32), "vv": ("sbuf", [128, 3, K], BF),
@@ -140,42 +142,46 @@ def rank_program(g, core, T, topo):
         op(q, lambda: eng.dma_start(dst, src).then_inc(T.sem[sem], 16), [], [key], (sem, 16))
 
     load("S", Y, T.d0[:], T.wk[:], "l_wk", "d0")
-    load("S", Y, T.b0s[:], T.b0[:], "l_b0", "b0s")
-    load("A", S, T.recs[:], T.rec[:], "l_rec", "recs")
+    load("A", S, T.b0s[:], T.b0[:], "l_b0", "b0s")
+    load("S", Y, T.recs[:], T.rec[:], "l_rec", "recs")
     load("A", S, T.ws[:], T.w[:], "l_w", "ws")
-    op("V", lambda: V.memset(T.bd0[:], 2.0 ** 46), [], ["bd0"])
+    TB = ["tbL", "tbR"]
+    cut = 1360
+    op("V", lambda: V.memset(T.zin[:, 0:64], -128.0), [], ["zin0"])
+    op("V", lambda: V.memset(T.tb[:, 0:cut], 0), [], ["tbL"])
+    op("G", lambda: g.iota(T.tb[:, cut:W], [[0, W - cut]], 0, 0), [], ["tbR"])
+    op("G", lambda: g.dma_start(T.ths[:, 0:1], T.th[:], allow_slow_non_contiguous=True).then_inc(T.sem.l_th, 16),
+       [], ["ths"], ("l_th", 16))
     op("V", lambda: V.memset(T.ones[:], 1.0), [], ["ones"])
-    op("V", lambda: V.memset(T.zin[:], -128.0), [], ["zin"])
-    op("V", lambda: V.memset(T.tb[:], 0), [], ["tb"])
+    op("V", lambda: V.memset(T.bd0[:], 2.0 ** 46), [], ["bd0"])
+    op("V", lambda: V.memset(T.zin[:, 64:K], -128.0), [], ["zin"])
     op("V", lambda: V.memset(T.sel[:], 0.0), [], ["sel"])
 
     def tables():
         for t in range(5):
             src = T.hop[:, t * W:(t + 1) * W] if t < 3 else (T.up[:] if t == 3 else T.dn[:])
             Y.dma_start(T.tb[ROW0 + ROWS * t::16, :], src).then_inc(T.sem.l_tb, 16)
-    op("S", tables, [], ["tb"], ("l_tb", 80))
+    op("S", tables, [], TB, ("l_tb", 80))
 
     op("G", lambda: g.affine_select(T.jj[:], T.ones[:], [[1, 160]], A.is_equal, 0.0, -16, -1), ["ones"], ["jj"])
     op("G", lambda: g.affine_select(T.bd1[:], T.bd0[:], [[-16, 8], [0, 16]], A.is_ge, 0.0, 0, 1), ["bd0"], ["bd1"])
     op("G", lambda: g.affine_select(T.pe[:], T.jj[:], [[0, 5], [1, 2], [0, 16]], A.is_gt, 0.0, 0, 0), ["jj"], ["pe"])
     op("G", lambda: g.affine_select(T.po[:], T.jj[:], [[0, 5], [1, 2], [0, 16]], A.is_equal, 0.0, 0, 0), ["jj"], ["po"])
     op("G", lambda: g.affine_select(T.bda[:], T.bd1[:], [[16, 8], [0, 16]], A.is_ge, 0.0, 15, -1), ["bd1"], ["bda"])
-    op("G", lambda: g.dma_start(T.ths[:, 0:1], T.th[:], allow_slow_non_contiguous=True).then_inc(T.sem.l_th, 16),
-       [], ["ths"], ("l_th", 16))
 
     def gfill(ap, cols, val, key):
         op("G", lambda: g.iota(ap, [[0, cols]], val, 0, allow_small_or_imprecise_dtypes=True), [], [key])
-    gfill(T.cc[:, W // 2:W], W // 2, 0, "cR")
-    for j in range(2):
-        op("A", lambda j=j: S.activation(T.cc[:, j * K:(j + 1) * K], T.zin[:], Fn.Silu), ["zin"], ["cL"])
+    op("A", lambda: S.activation(T.cc[:, 0:64], T.zin[:, 0:64], Fn.Silu), ["zin0"], ["cL"])
     op("A", lambda: S.activation(T.bb[:], T.b0s[:], Fn.Copy), ["b0s"], ["bb"])
     op("V", lambda: V.tensor_copy(T.d16[:], T.d0[:]), ["d0"], ["d16"])
 
     def zero_b():
-        op("A", lambda: S.activation(win("bb", T.d16[:]), T.zin[:], Fn.Silu), ["zin", "d16"], ["bb"])
+        op("A", lambda: S.activation(win("bb", T.d16[:]), T.zin[:], Fn.Silu), ["zin0", "zin", "d16"], ["bb"])
 
     def table_gather():
-        op("V", lambda: V.tensor_copy(T.tg[:], win("tb", T.d16[:])), ["tb", "d16"], ["tg"])
+        op("V", lambda: V.tensor_copy(T.tg[:], win("tb", T.d16[:])), TB + ["d16"], ["tg"])
+
+    def table_turn():
         op("V", lambda: V.transpose(T.tr[:], T.tg[:]), ["tg"], ["tr"])
 
         def sort_groups():
@@ -210,12 +216,16 @@ def rank_program(g, core, T, topo):
             Y.dma_start(T["lr%d" % s][0:16, :], T["lu%d" % s][112:128, :]).then_inc(T.sem["rot%d" % s], 16)
         op("S", turn, ["lu%d" % s], ["lr%d" % s], ("rot%d" % s, 32))
 
-    def c_scatter(s, a, b):
+    def c_scatter(s, i):
+        a, b = CUTS[s][i], CUTS[s][i + 1]
+        if a == b:
+            return
         lst = T.d16[:, a // 16:b // 16]
         if s == 0:
             op("V", lambda: V.tensor_copy(win("cc", lst), T.dl[:, a:b]), ["dl", "d16"], C2)
         else:
-            op("V", lambda: V.tensor_tensor(win("cc", lst), T.cd[:, a:b], T.dl[:, a:b], A.add), ["dl", "cd%d" % a, "d16"], C2)
+            op("V", lambda: V.tensor_tensor(win("cc", lst), T.cd[:, a:b], T.dl[:, a:b], A.add),
+               ["dl", "d16", "cd0"] + (["cd%d" % H] if b > H else []), C2)
 
     def c_gather(a, b):
         op("A", lambda: S.activation(T.cd[:, a:b], win("cc", T.d16[:, a // 16:b // 16]), Fn.Copy), C2 + ["d16"], ["cd%d" % a])
@@ -240,24 +250,26 @@ def rank_program(g, core, T, topo):
         par = (5 * s + k) % 2
         return "pa%d" % par, "pb%d" % par
 
-    def over(s, k, opens=True):
+    def size(k):
         gb = "g%d" % (k % 3)
-        pa, pb = banks(s, k)
         op("A", lambda: S.activation(T.ag[:], T[gb][:], Fn.Abs), [gb], ["ag"])
+
+    def over(s, k, opens=True):
+        pa, pb = banks(s, k)
         op("A", lambda: S.activation(T.rl[:], T.ag[:], Fn.Relu, bias=T.nth[:, 0:1]), ["ag", "nth"], ["rl"])
         op("A", lambda: S.activation(T.ov[:], T.rl[:], Fn.Sign), ["rl"], ["ov"])
 
         def count():
-            P.matmul(T[pa][:, 0:H], T.bdb[:], T.ov[:, 0:H], opens, not opens)
-            return P.matmul(T[pb][:, 0:H], T.bdb[:], T.ov[:, H:K], opens, not opens)
+            P.matmul(T[pa][:, 0:MA], T.bdb[:], T.ov[:, 0:MA], opens, not opens)
+            return P.matmul(T[pb][:, 0:K - MA], T.bdb[:], T.ov[:, MA:K], opens, not opens)
         op("P", count, ["ov", "bdb"], [pa, pb])
 
     def empty(s, k, opens=False):
         lst, lk, _h, _hk = arrival(s, k)
         pa, pb = banks(s, k)
         op("A", lambda: S.activation(T.ab[:], win("bb", lst), Fn.Abs, scale=2.0 ** 64), ["bb", lk], ["ab"])
-        op("P", lambda: P.matmul(T[pa][:, 0:H], T.bda[:], T.ab[:, 0:H], opens, not opens), ["ab", "bda"], [pa])
-        op("P", lambda: P.matmul(T[pb][:, 0:H], T.bda[:], T.ab[:, H:K], opens, not opens), ["ab", "bda"], [pb])
+        op("P", lambda: P.matmul(T[pb][:, 0:K - MA], T.bda[:], T.ab[:, MA:K], opens, not opens), ["ab", "bda"], [pb])
+        op("P", lambda: P.matmul(T[pa][:, 0:MA], T.bda[:], T.ab[:, 0:MA], opens, not opens), ["ab", "bda"], [pa])
 
     def make_sum(s, k):
         lst, lk, _h, _hk = arrival(s, k)
@@ -266,15 +278,15 @@ def rank_program(g, core, T, topo):
 
     def mask_b(s, k):
         pb = banks(s, k)[1]
-        op("A", lambda: S.activation(T.mt[:], T[pb][:, 0:H], Fn.Relu, bias=-THR), [pb], ["mt"])
-        op("A", lambda: S.activation(T.mk[:, H:K], T.mt[:], Fn.Sign), ["mt"], ["mkB"])
+        op("A", lambda: S.activation(T.mt[:], T[pb][:, 0:K - MA], Fn.Relu, bias=-THR), [pb], ["mt"])
+        op("A", lambda: S.activation(T.mk[:, MA:K], T.mt[:], Fn.Sign), ["mt"], ["mkB"])
 
     def put(s, k, both):
         lst, lk, _h, _hk = arrival(s, k)
         pa, pb = banks(s, k)
-        op("V", lambda: V.tensor_scalar(T.mk[:, 0:H], T[pa][:, 0:H], THR, None, A.is_gt), [pa], ["mkA"])
         if both:
-            op("V", lambda: V.tensor_scalar(T.mk[:, H:K], T[pb][:, 0:H], THR, None, A.is_gt), [pb], ["mkB"])
+            op("V", lambda: V.tensor_scalar(T.mk[:, MA:K], T[pb][:, 0:K - MA], THR, None, A.is_gt), [pb], ["mkB"])
+        op("V", lambda: V.tensor_scalar(T.mk[:, 0:MA], T[pa][:, 0:MA], THR, None, A.is_gt), [pa], ["mkA"])
         op("V", lambda: V.tensor_tensor(win("bb", lst), T.sm[:], T.mk[:], A.mult), ["sm", "mkA", "mkB", lk], ["bb"])
 
     def keys():
@@ -291,23 +303,44 @@ def rank_program(g, core, T, topo):
                 op("A", lambda k=k, lst=lst, a=a, b=b: S.activation(T.mm[:, k, a:b], win("bb", lst), Fn.Abs),
                    ["bb", "x%d" % k], ["m%d%d" % (k, hf)])
         op("A", lambda: S.activation(win("held", T.d16[:]), T["sh%d" % s][:], Fn.Silu), ["sh%d" % s, "d16"], ["held"])
-        for hf in range(2):
-            a, b = hf * H, (hf + 1) * H
-            op("V", lambda a=a, b=b: V.tensor_tensor(T.pm[:, a:b], T.mm[:, 0, a:b], T.mm[:, 1, a:b], A.max),
-               ["m0%d" % hf, "m1%d" % hf], ["pm%d" % hf])
-            op("V", lambda a=a, b=b: V.tensor_tensor(T.pm[:, a:b], T.pm[:, a:b], T.mm[:, 2, a:b], A.max),
-               ["pm%d" % hf, "m2%d" % hf], ["pm%d" % hf])
-            for k in range(3):
-                op("V", lambda k=k, a=a, b=b: V.tensor_tensor(T.vv[:, k, a:b], T.pm[:, a:b], T.mm[:, k, a:b], A.is_equal),
-                   ["pm%d" % hf, "m%d%d" % (k, hf)], ["v%d%d" % (k, hf)])
 
-            def votes(hf=hf, a=a, b=b):
+        def max01(hf):
+            a, b = hf * H, (hf + 1) * H
+            op("V", lambda: V.tensor_tensor(T.pm[:, a:b], T.mm[:, 0, a:b], T.mm[:, 1, a:b], A.max),
+               ["m0%d" % hf, "m1%d" % hf], ["pm%d" % hf])
+
+        def max2(hf):
+            a, b = hf * H, (hf + 1) * H
+            op("V", lambda: V.tensor_tensor(T.pm[:, a:b], T.pm[:, a:b], T.mm[:, 2, a:b], A.max),
+               ["pm%d" % hf, "m2%d" % hf], ["pm%d" % hf])
+
+        def vote(hf, k):
+            a, b = hf * H, (hf + 1) * H
+            op("V", lambda: V.tensor_tensor(T.vv[:, k, a:b], T.pm[:, a:b], T.mm[:, k, a:b], A.is_equal),
+               ["pm%d" % hf, "m%d%d" % (k, hf)], ["v%d%d" % (k, hf)])
+
+        def votes(hf):
+            a, b = hf * H, (hf + 1) * H
+
+            def fn():
                 last = None
                 for i in range(16):
                     last = P.matmul(T.pv[:, 0:3, 16 * hf:16 * hf + 16], T.sel[:, 15 - i:143 - i], T.vv[:, :, a + i:b:16],
                                     i == 0, i == 15)
                 return last
-            op("P", votes, ["sel", "v0%d" % hf, "v1%d" % hf, "v2%d" % hf], ["pv"])
+            op("P", fn, ["sel", "v0%d" % hf, "v1%d" % hf, "v2%d" % hf], ["pv"])
+        max01(0)
+        max2(0)
+        vote(0, 0)
+        vote(0, 1)
+        max01(1)
+        vote(0, 2)
+        votes(0)
+        max2(1)
+        for k in range(3):
+            vote(1, k)
+        votes(1)
+        c_scatter(s, 3)
         op("V", lambda: V.tensor_tensor(T.key[:], T.pv[:, 0:3, :], T.xk[:], A.add), ["pv", "xk"], ["key"])
         op("V", lambda: V.tensor_tensor(T.k01[:], T.key[:, 0, :], T.key[:, 1, :], A.max), ["key"], ["k01"])
         op("V", lambda: V.tensor_tensor(T.kk[:], T.k01[:], T.key[:, 2, :], A.max), ["key", "k01"], ["kk"])
@@ -358,9 +391,11 @@ def rank_program(g, core, T, topo):
             c_gather(0, H)
             table_gather()
             op("V", lambda: V.tensor_tensor(T.dl[:], win("recs", T.d16[:]), T.nb[:], A.mult), ["recs", "d16", "nb"], ["dl"])
+        table_turn()
         op("V", lambda h=h: V.tensor_tensor(h, win("ws", T.d16[:]), T.dl[:], A.mult), ["ws", "d16", "dl"], [hk])
         lists_and_send(s)
         if s == 0:
+            gfill(T.cc[:, 64:W], W - 64, 0, "cR")
             gfill(T.held[:], W, 0, "held")
             gfill(T.sh0[:], K, 32, "sh0")
             gfill(T.sf0[:], K, 1, "sf0")
@@ -369,27 +404,28 @@ def rank_program(g, core, T, topo):
             gfill(T.sf1[:], K, 16, "sf1")
         last = s == RO - 1
         empty(s, 0, True)
-        make_g(s, 0)
-        over(s, 0, False)
         hop_list(1)
-        hop_list(2)
+        make_g(s, 0)
+        size(0)
+        over(s, 0, False)
         make_g(s, 1)
+        hop_list(2)
         make_sum(s, 0)
-        if last:
-            c_scatter(s, 0, H)
+        c_scatter(s, 0)
         for k in range(5):
             if k > 0:
                 empty(s, k)
-                make_sum(s, k)
                 if k < 4:
                     make_g(s, k + 1)
+                make_sum(s, k)
             if k < 4:
+                size(k + 1)
                 mask_b(s, k)
             elif last:
-                c_scatter(s, H, K)
+                c_scatter(s, 1)
                 op("S", lambda: Y.dma_start(T.yc[:], T.cc[:]).then_inc(T.sem.o_c, 16), C2, ["yc"], ("o_c", 16))
             else:
-                c_scatter(s, 0, H)
+                c_scatter(s, 1)
             put(s, k, k == 4)
             if k < 4:
                 over(s, k + 1)
@@ -398,7 +434,7 @@ def rank_program(g, core, T, topo):
             if k == 1 and s > 0:
                 c_gather(H, K)
         if not last:
-            c_scatter(s, H, K)
+            c_scatter(s, 2)
             election(s)
 
     op("S", lambda: Y.dma_start(T.yb[:], T.bb[:]).then_inc(T.sem.o_b, 16), ["bb"], ["yb"], ("o_b", 16))

@@ -3,47 +3,61 @@ from concourse.mybir import AluOpType, ActivationFunctionType
 W, K, RO = 2048, 512, 3
 F32, BF, F16, I32, U16 = "float32", "bfloat16", "float16", "int32", "uint16"
 MSG = K + 64
-MA = 384
-CUTS = [[0, 0, 192, 352, 512], [0, 128, 256, 384, 512], [0, 256, 512]]
+H = K // 2
+MA = [512, 256, 256, 256, 192]
+CUTS = [[0, 0, 0, 64, 160, 256, 416, 512], [0, 0, 0, 64, 160, 256, 416, 512], [0, 128, 256, 512]]
+SLA = True
+SPLIT = [4]
+MODE = 1
+SQ = 0
+CG = {0: (0, 256), 1: (256, 512)}
+EARLY = [0, 1, 0]
+EL = 192
+TBV = 1536
+CPG = 0
 ROW0, ROWS = 0, 3
-THR = 8.5 * 2.0 ** -20
+UNIT = 2.0 ** -20
+TOP = 2.0 - 2.0 ** -13
 SELW = 8192.0
+X0 = 448
+MARK = (32, 512)
 
 SCRATCH = {
     "bb": ("sbuf", [128, W], F32), "cc": ("sbuf", [128, W], F32), "held": ("sbuf", [128, W], F32),
-    "tb": ("sbuf", [128, W], I32), "first": ("sbuf", [128, 3 * W], BF),
+    "tb": ("sbuf", [128, W], I32), "st": ("sbuf", [128, 3 * W + 8], F32),
     "b0s": ("sbuf", [128, W], BF), "ws": ("sbuf", [128, W], BF), "recs": ("sbuf", [128, W], BF),
-    "ths": ("sbuf", [128, 8], F32), "nth": ("sbuf", [128, 8], F32),
+    "ths": ("sbuf", [128, 8], F32), "aux": ("sbuf", [128, 8], F32), "rough": ("sbuf", [128, 16], BF),
+    "sc": ("sbuf", [128, 8], F32), "lim": ("sbuf", [128, 8], F32),
     "zin": ("sbuf", [128, K], F32), "sh0": ("sbuf", [128, K], F32), "sh1": ("sbuf", [128, K], F32),
-    "sf0": ("sbuf", [128, K], BF), "sf1": ("sbuf", [128, K], BF),
     "ones": ("sbuf", [128, 160], F32), "jj": ("sbuf", [128, 160], F32),
     "pe": ("sbuf", [128, 160], F16), "po": ("sbuf", [128, 160], F16),
-    "bd0": ("sbuf", [128, 128], BF), "bd1": ("sbuf", [128, 128], BF), "bda": ("sbuf", [128, 128], BF),
-    "bdb": ("sbuf", [128, 128], BF), "sel": ("sbuf", [128, 144], BF),
-    "d0": ("sbuf", [128, 32], I32), "d1": ("sbuf", [128, 32], I32), "d2": ("sbuf", [128, 32], I32),
-    "d16": ("sbuf", [128, 32], U16), "xl": ("sbuf", [128, 96], U16), "xu": ("sbuf", [128, 32], U16),
-    "xd": ("sbuf", [128, 32], U16), "lw16": ("sbuf", [128, 64], U16),
+    "bd0": ("sbuf", [128, 2, 128], BF), "bd1": ("sbuf", [128, 2, 128], BF), "bd": ("sbuf", [128, 2, 128], BF),
+    "sel": ("sbuf", [128, 144], BF), "seln": ("sbuf", [128, 144], BF),
+    "one": ("sbuf", [128, 128], BF), "kc": ("sbuf", [128, 96], BF), "pat": ("sbuf", [128, 96], BF),
+    "d0": ("sbuf", [128, 32], I32), "e0": ("sbuf", [128, 32], U16), "e1": ("sbuf", [128, 32], U16),
+    "e2": ("sbuf", [128, 32], U16),
+    "x0": ("sbuf", [128, 32], U16), "x12": ("sbuf", [128, 64], U16), "xu": ("sbuf", [128, 32], U16),
+    "xd": ("sbuf", [128, 32], U16), "lw16": ("sbuf", [128, 64], U16), "l1": ("sbuf", [128, 32], U16),
+    "l2": ("sbuf", [128, 32], U16),
     "nb": ("sbuf", [128, K], F32), "dl": ("sbuf", [128, K], F32), "cd": ("sbuf", [128, K], F32),
     "tg": ("sbuf", [128, K], F16), "tr": ("sbuf", [128, 16, 2, 16], F16),
     "g0": ("sbuf", [128, K], F32), "g1": ("sbuf", [128, K], F32), "g2": ("sbuf", [128, K], F32),
-    "sm": ("sbuf", [128, K], F32), "mk": ("sbuf", [128, K], F32), "mt": ("sbuf", [128, K - MA], F32),
+    "sm": ("sbuf", [128, K], F32), "mk": ("sbuf", [128, K], F32), "cr": ("sbuf", [128, K], BF),
     "ag": ("sbuf", [128, K], F32), "rl": ("sbuf", [128, K], F32), "ov": ("sbuf", [128, K], BF),
     "ab": ("sbuf", [128, K], BF),
-    "mm": ("sbuf", [128, 3, K], F32), "vv": ("sbuf", [128, 3, K], BF),
-    "xk": ("sbuf", [128, 3, 32], F32), "key": ("sbuf", [128, 3, 32], I32), "k01": ("sbuf", [128, 32], I32),
-    "kk": ("sbuf", [128, 32], I32), "lw": ("sbuf", [128, 64], I32), "rr": ("sbuf", [128, 32], I32),
-    "thr": ("sbuf", [128, 32], F32), "dif": ("sbuf", [128, 32], I32), "tt": ("sbuf", [128, 32], F32),
-    "go": ("sbuf", [128, 32], I32), "dd": ("sbuf", [128, 32], I32),
-    "hg": ("sbuf", [128, K], BF), "lk": ("sbuf", [128, 2, K], BF),
+    "mm": ("sbuf", [128, 3, K], F32), "vv": ("sbuf", [128, K, 3], BF),
+    "ks": ("sbuf", [128, 96], I32), "lw": ("sbuf", [128, 64], I32),
+    "bs": ("sbuf", [128, 96], F32), "dn0": ("sbuf", [128, 96], F32), "dn1": ("sbuf", [128, 96], F32),
+    "hg": ("sbuf", [128, K], BF), "lk": ("sbuf", [128, K, 3], BF),
     "pa0": ("psum", [128, K], F32), "pb0": ("psum", [128, K], F32),
     "pa1": ("psum", [128, K], F32), "pb1": ("psum", [128, K], F32),
-    "pl": ("psum", [128, 32, 16], F32), "pm": ("psum", [128, K], F32),
-    "pv": ("psum", [128, 16, 32], F32), "pk": ("psum", [128, 16, 32], F32),
+    "pc": ("psum", [128, K], F32), "pm": ("psum", [128, K], F32),
+    "pl": ("psum", [128, 256, 2], F32), "pv": ("psum", [128, K], F32),
 }
 for _s in range(RO):
     for _n in ("snd", "lu", "lr", "ld"):
         SCRATCH["%s%d" % (_n, _s)] = ("sbuf", [128, MSG], F32)
-PSUM = ("pa0", "pb0", "pa1", "pb1", "pl", "pm", "pv", "pk")
+PSUM = ("pa0", "pb0", "pa1", "pb1", "pc", "pl", "pm", "pv")
 
 SEMAPHORES = ["cV", "cA", "cP", "cG", "l_wk", "l_th", "l_b0", "l_rec", "l_w", "l_tb", "sent", "o_c", "o_b"]
 for _s in range(RO):
@@ -130,7 +144,7 @@ def rank_program(g, core, T, topo):
     V, S, P, Y = g.vector, g.scalar, g.tensor, g.sync
     plan = new_plan()
     C2 = ["cL", "cR"]
-    H = K // 2
+    BB = ["bb", "bbG"]
 
     def op(q, fn, reads=(), writes=(), dma=None):
         return add(plan, q, fn, reads, writes, dma)
@@ -138,24 +152,27 @@ def rank_program(g, core, T, topo):
     def win(name, lst, a=0, b=W):
         return T[name][:, a:b].indirect(lst)
 
+    def part(name, a=0, b=K):
+        return ["%s_%d" % (name, i) for i in range(a // 64, (b + 63) // 64)]
+
     def load(q, eng, dst, src, sem, key):
         op(q, lambda: eng.dma_start(dst, src).then_inc(T.sem[sem], 16), [], [key], (sem, 16))
 
-    load("S", Y, T.d0[:], T.wk[:], "l_wk", "d0")
     load("A", S, T.b0s[:], T.b0[:], "l_b0", "b0s")
+    load("S", Y, T.d0[:], T.wk[:], "l_wk", "d0")
     load("S", Y, T.recs[:], T.rec[:], "l_rec", "recs")
-    load("A", S, T.ws[:], T.w[:], "l_w", "ws")
+    load("S", Y, T.ws[:], T.w[:], "l_w", "ws")
     TB = ["tbL", "tbR"]
-    cut = 1360
     op("V", lambda: V.memset(T.zin[:, 0:64], -128.0), [], ["zin0"])
-    op("V", lambda: V.memset(T.tb[:, 0:cut], 0), [], ["tbL"])
-    op("G", lambda: g.iota(T.tb[:, cut:W], [[0, W - cut]], 0, 0), [], ["tbR"])
+    op("V", lambda: V.memset(T.tb[:, 0:TBV], 0), [], ["tbL"])
+    op("V", lambda: V.memset(T.ones[:], 1.0), [], ["ones"])
     op("G", lambda: g.dma_start(T.ths[:, 0:1], T.th[:], allow_slow_non_contiguous=True).then_inc(T.sem.l_th, 16),
        [], ["ths"], ("l_th", 16))
-    op("V", lambda: V.memset(T.ones[:], 1.0), [], ["ones"])
-    op("V", lambda: V.memset(T.bd0[:], 2.0 ** 46), [], ["bd0"])
+    op("G", lambda: g.iota(T.tb[:, TBV:W], [[0, W - TBV]], 0, 0), [], ["tbR"])
+    op("V", lambda: V.memset(T.bd0[:, 0, :], 2.0 ** 46), [], ["bd0a"])
+    op("V", lambda: V.memset(T.bd0[:, 1, :], UNIT), [], ["bd0b"])
+    bda, bdb = T.bd[:, 0, :], T.bd[:, 1, :]
     op("V", lambda: V.memset(T.zin[:, 64:K], -128.0), [], ["zin"])
-    op("V", lambda: V.memset(T.sel[:], 0.0), [], ["sel"])
 
     def tables():
         for t in range(5):
@@ -164,50 +181,101 @@ def rank_program(g, core, T, topo):
     op("S", tables, [], TB, ("l_tb", 80))
 
     op("G", lambda: g.affine_select(T.jj[:], T.ones[:], [[1, 160]], A.is_equal, 0.0, -16, -1), ["ones"], ["jj"])
-    op("G", lambda: g.affine_select(T.bd1[:], T.bd0[:], [[-16, 8], [0, 16]], A.is_ge, 0.0, 0, 1), ["bd0"], ["bd1"])
+    op("G", lambda: g.affine_select(T.bd1[:], T.bd0[:], [[0, 2], [-16, 8], [0, 16]], A.is_ge, 0.0, 0, 1),
+       ["bd0a", "bd0b"], ["bd1"])
     op("G", lambda: g.affine_select(T.pe[:], T.jj[:], [[0, 5], [1, 2], [0, 16]], A.is_gt, 0.0, 0, 0), ["jj"], ["pe"])
     op("G", lambda: g.affine_select(T.po[:], T.jj[:], [[0, 5], [1, 2], [0, 16]], A.is_equal, 0.0, 0, 0), ["jj"], ["po"])
-    op("G", lambda: g.affine_select(T.bda[:], T.bd1[:], [[16, 8], [0, 16]], A.is_ge, 0.0, 15, -1), ["bd1"], ["bda"])
+    if CPG:
+        op("G", lambda: g.affine_select(T.bb[:, W - CPG:W], T.b0s[:, W - CPG:W], [[0, CPG]], A.is_equal, 0.0, 0, 0),
+           ["b0s"], ["bbG"])
+    op("G", lambda: g.affine_select(T.bd[:], T.bd1[:], [[0, 2], [16, 8], [0, 16]], A.is_ge, 0.0, 15, -1), ["bd1"], ["bd"])
 
-    def gfill(ap, cols, val, key):
-        op("G", lambda: g.iota(ap, [[0, cols]], val, 0, allow_small_or_imprecise_dtypes=True), [], [key])
+    def gfill(ap, pattern, val, keys):
+        op("G", lambda: g.iota(ap, pattern, val, 0, allow_small_or_imprecise_dtypes=True), [], keys)
+
+    def gkeep(name, pattern, test, base, mult):
+        op("G", lambda: g.affine_select(T[name][:], T[name][:], pattern, test, 0.0, base, mult), [name], [name])
     op("A", lambda: S.activation(T.cc[:, 0:64], T.zin[:, 0:64], Fn.Silu), ["zin0"], ["cL"])
-    op("A", lambda: S.activation(T.bb[:], T.b0s[:], Fn.Copy), ["b0s"], ["bb"])
-    op("V", lambda: V.tensor_copy(T.d16[:], T.d0[:]), ["d0"], ["d16"])
+    op("A", lambda: S.activation(T.bb[:, 0:W - CPG], T.b0s[:, 0:W - CPG], Fn.Copy), ["b0s"], ["bb"])
+    op("V", lambda: V.tensor_copy(T.e0[:], T.d0[:]), ["d0"], ["e0"])
 
-    def zero_b():
-        op("A", lambda: S.activation(win("bb", T.d16[:]), T.zin[:], Fn.Silu), ["zin0", "zin", "d16"], ["bb"])
+    def limit(i):
+        th, c = T.ths[:, 0:1], lambda j: T.aux[:, j:j + 1]
+        if i == 0:
+            op("V", lambda: V.reciprocal(c(0), th), ["ths"], ["aux0"])
+        if i == 1:
+            op("V", lambda: V.tensor_scalar(T.rough[:, 0:1], c(0), TOP, None, A.mult), ["aux0"], ["rough"])
+            op("V", lambda: V.tensor_scalar(c(1), c(0), TOP, None, A.mult), ["aux0"], ["aux1"])
+        if i == 2:
+            op("V", lambda: V.tensor_scalar(c(2), th, T.rough[:, 0:1], 2.0, A.mult, A.is_lt), ["ths", "rough"], ["aux2"])
+        if i == 3:
+            op("V", lambda: V.tensor_scalar(T.sc[:, 0:1], T.rough[:, 0:1], c(2), c(1), A.mult, A.max),
+               ["aux1", "aux2", "rough"], ["sc"])
+        if i == 4:
+            op("A", lambda: S.activation(c(3), th, Fn.Square, scale=T.sc[:, 0:1]), ["ths", "sc"], ["aux3"])
+            op("A", lambda: S.activation(T.lim[:, 0:1], c(3), Fn.Identity, bias=-2.0 ** -22, scale=-1.0), ["aux3"], ["lim"])
 
-    def table_gather():
-        op("V", lambda: V.tensor_copy(T.tg[:], win("tb", T.d16[:])), TB + ["d16"], ["tg"])
+    def take_b(s, a, b):
+        e = T["e%d" % s][:, a // 16:b // 16]
+        if s == 0:
+            op("V", lambda: V.tensor_scalar(T.nb[:, a:b], win("b0s", e), -1.0, None, A.mult), ["b0s", "e0"], part("nb", a, b))
+        else:
+            op("A", lambda: S.activation(T.nb[:, a:b], win("bb", e), Fn.Copy, scale=-1.0), ["bb", "e%d" % s], part("nb", a, b))
 
-    def table_turn():
-        op("V", lambda: V.transpose(T.tr[:], T.tg[:]), ["tg"], ["tr"])
+    def zero_b(s):
+        op("A", lambda: S.activation(win("bb", T["e%d" % s][:]), T.zin[:], Fn.Silu), ["zin0", "zin", "e%d" % s], BB)
 
-        def sort_groups():
+    def delta(s, a, b):
+        e = T["e%d" % s][:, a // 16:b // 16]
+        op("V", lambda: V.tensor_tensor(T.dl[:, a:b], win("recs", e), T.nb[:, a:b], A.mult),
+           ["recs", "e%d" % s] + part("nb", a, b), part("dl", a, b))
+
+    def make_h(s, a, b):
+        e = T["e%d" % s][:, a // 16:b // 16]
+        op("V", lambda: V.tensor_tensor(T["snd%d" % s][:, a:b], win("ws", e), T.dl[:, a:b], A.mult),
+           ["ws", "e%d" % s] + part("dl", a, b), part("h%d" % s, a, b))
+
+    def table_gather(s):
+        op("V", lambda: V.tensor_copy(T.tg[:], win("tb", T["e%d" % s][:])), TB + ["e%d" % s], ["tg"])
+
+    def sort_groups(out, t0, t1, key, opens=True):
+        def fn():
             last = None
             for cp in range(2):
                 m = T.pe if cp == 0 else T.po
                 for gp in range(2):
                     a = 16 - 16 * (gp - cp)
-                    last = P.matmul(T.pl[:, cp::2, 0:5], m[:, a:a + 128],
-                                    T.tr[:, :, gp, ROW0:ROW0 + 4 * ROWS + 1:ROWS], gp == 0, gp == 1)
+                    r0 = ROW0 + ROWS * t0
+                    rhs = T.tr[:, :, gp, r0] if t1 == t0 + 1 else T.tr[:, :, gp, r0:r0 + (t1 - t0 - 1) * ROWS + 1:ROWS]
+                    last = P.matmul(out(cp), m[:, a:a + 128], rhs, opens and gp == 0, opens and gp == 1)
             return last
-        op("P", sort_groups, ["tr", "pe", "po"], ["pl"])
+        op("P", fn, ["tr", "pe", "po"], [key])
 
-    def hop_list(k):
-        op("V", lambda: V.tensor_copy(T.xl[:, 32 * k:32 * k + 32], T.pl[:, :, k]), ["pl"], ["x%d" % k])
+    def table_turn():
+        op("V", lambda: V.transpose(T.tr[:], T.tg[:]), ["tg"], ["tr"])
+        sort_groups(lambda cp: T.pc[:, X0 + cp:X0 + 32:2], 0, 1, "pc")
+        sort_groups(lambda cp: T.pl[:, cp:32:2, :], 3, 5, "pl")
+        for t in (1, 2):
+            sort_groups(lambda cp, t=t: T.pm[:, 32 * t - 32 + cp:32 * t:2], t, t + 1, "pm")
 
-    def lists_and_send(s):
+    def list0():
+        op("V", lambda: V.tensor_copy(T.x0[:], T.pc[:, X0:X0 + 32]), ["pc"], ["x0"])
+
+    def list12():
+        op("V", lambda: V.tensor_copy(T.x12[:], T.pm[:, 0:64]), ["pm"], ["x12"])
+
+    def send(s):
         snd = T["snd%d" % s]
-        hop_list(0)
-        op("V", lambda: V.tensor_copy(snd[:, K:MSG], T.pl[:, :, 3:5]), ["pl"], ["sl%d" % s])
+        if SLA:
+            op("A", lambda: S.activation(snd[:, K:MSG], T.pl[:, 0:32, :], Fn.Copy), ["pl"], ["sl%d" % s])
+        else:
+            op("V", lambda: V.tensor_copy(snd[:, K:MSG], T.pl[:, 0:32, :]), ["pl"], ["sl%d" % s])
         for dst, land, sem in ((T.cores[(rank + 1) % n], "lu", "au"), (T.cores[(rank - 1) % n], "ld", "ad")):
-            def send(dst=dst, land=land, sem=sem):
+            def write(dst=dst, land=land, sem=sem):
                 rid, pid, _e = topo.addr(dst)
                 g.remote_dma(T["%s%d" % (land, s)][:], snd[:], T.sem["%s%d" % (sem, s)], T.sem.sent, pid, rid,
                              topo.mask(core, dst))
-            op("G", send, ["h%d" % s, "sl%d" % s], [], ("sent", 0))
+            op("G", write, part("h%d" % s) + ["sl%d" % s], [], ("sent", 0))
         op(None, None, [], ["lu%d" % s], ("au%d" % s, len(topo.engines(T.cores[(rank - 1) % n], core))))
         op(None, None, [], ["ld%d" % s], ("ad%d" % s, len(topo.engines(T.cores[(rank + 1) % n], core))))
 
@@ -217,119 +285,152 @@ def rank_program(g, core, T, topo):
         op("S", turn, ["lu%d" % s], ["lr%d" % s], ("rot%d" % s, 32))
 
     def c_scatter(s, i):
-        a, b = CUTS[s][i], CUTS[s][i + 1]
-        if a == b:
+        if i + 1 >= len(CUTS[s]) or CUTS[s][i] == CUTS[s][i + 1]:
             return
-        lst = T.d16[:, a // 16:b // 16]
+        a, b = CUTS[s][i], CUTS[s][i + 1]
+        lst, ek = T["e%d" % s][:, a // 16:b // 16], "e%d" % s
         if s == 0:
-            op("V", lambda: V.tensor_copy(win("cc", lst), T.dl[:, a:b]), ["dl", "d16"], C2)
+            op("V", lambda: V.tensor_copy(win("cc", lst), T.dl[:, a:b]), part("dl", a, b) + [ek], C2)
         else:
             op("V", lambda: V.tensor_tensor(win("cc", lst), T.cd[:, a:b], T.dl[:, a:b], A.add),
-               ["dl", "d16", "cd0"] + (["cd%d" % H] if b > H else []), C2)
+               part("dl", a, b) + part("cd", a, b) + [ek], C2)
 
-    def c_gather(a, b):
-        op("A", lambda: S.activation(T.cd[:, a:b], win("cc", T.d16[:, a // 16:b // 16]), Fn.Copy), C2 + ["d16"], ["cd%d" % a])
+    def c_gather(s, a, b):
+        op("A", lambda: S.activation(T.cd[:, a:b], win("cc", T["e%d" % s][:, a // 16:b // 16]), Fn.Copy),
+           C2 + ["e%d" % s], part("cd", a, b))
 
-    def arrival(s, k):
+    def arrival(s, k, a=0, b=K):
+        a16, b16 = a // 16, b // 16
         if k < 3:
-            return T.xl[:, 32 * k:32 * k + 32], "x%d" % k, T["snd%d" % s][:, 0:K], "h%d" % s
+            lst = T.x0[:, a16:b16] if k == 0 else T.x12[:, 32 * k - 32 + a16:32 * k - 32 + b16]
+            return lst, "x0" if k == 0 else "x12", T["snd%d" % s][:, a:b], part("h%d" % s, a, b)
         if k == 3:
-            return T.xu[:], "xu", T["lr%d" % s][:, 0:K], "lr%d" % s
-        return T.xd[:], "xd", T["ld%d" % s][:, 0:K], "ld%d" % s
+            return T.xu[:, a16:b16], "xu", T["lr%d" % s][:, a:b], ["lr%d" % s]
+        return T.xd[:, a16:b16], "xd", T["ld%d" % s][:, a:b], ["ld%d" % s]
 
-    def make_g(s, k):
-        lst, lk, h, hk = arrival(s, k)
+    def far_list(s, k):
         if k == 3:
-            op("V", lambda: V.tensor_copy(T.xu[:], T["lr%d" % s][:, K:MSG:2]), [hk], ["xu"])
+            op("V", lambda: V.tensor_copy(T.xu[:], T["lr%d" % s][:, K:MSG:2]), ["lr%d" % s], ["xu"])
         if k == 4:
-            op("V", lambda: V.tensor_copy(T.xd[:], T["ld%d" % s][:, K + 1:MSG:2]), [hk], ["xd"])
+            op("V", lambda: V.tensor_copy(T.xd[:], T["ld%d" % s][:, K + 1:MSG:2]), ["ld%d" % s], ["xd"])
+
+    def make_g(s, k, a=0, b=K):
+        lst, lk, h, hk = arrival(s, k, a, b)
+        if k + 1 - EARLY[k - 3] == k + 1:
+            far_list(s, k)
         gb = "g%d" % (k % 3)
-        op("V", lambda: V.tensor_tensor(T[gb][:], win("ws", lst), h, A.mult), ["ws", lk, hk], [gb])
+        op("V", lambda: V.tensor_tensor(T[gb][:, a:b], win("ws", lst), h, A.mult), ["ws", lk] + hk, part(gb, a, b))
 
     def banks(s, k):
         par = (5 * s + k) % 2
         return "pa%d" % par, "pb%d" % par
 
-    def size(k):
+    def size(k, a=0, b=K):
         gb = "g%d" % (k % 3)
-        op("A", lambda: S.activation(T.ag[:], T[gb][:], Fn.Abs), [gb], ["ag"])
+        op("A", lambda: S.activation(T.ag[:, a:b], T[gb][:, a:b], Fn.Square, scale=T.sc[:, 0:1]),
+           part(gb, a, b) + ["sc"], part("ag", a, b))
 
-    def over(s, k, opens=True):
-        pa, pb = banks(s, k)
-        op("A", lambda: S.activation(T.rl[:], T.ag[:], Fn.Relu, bias=T.nth[:, 0:1]), ["ag", "nth"], ["rl"])
-        op("A", lambda: S.activation(T.ov[:], T.rl[:], Fn.Sign), ["rl"], ["ov"])
+    def over(a=0, b=K):
+        op("A", lambda: S.activation(T.ov[:, a:b], T.ag[:, a:b], Fn.Sign, bias=T.lim[:, 0:1]),
+           part("ag", a, b) + ["lim"], part("ov", a, b))
 
-        def count():
-            P.matmul(T[pa][:, 0:MA], T.bdb[:], T.ov[:, 0:MA], opens, not opens)
-            return P.matmul(T[pb][:, 0:K - MA], T.bdb[:], T.ov[:, MA:K], opens, not opens)
-        op("P", count, ["ov", "bdb"], [pa, pb])
+    def count_b(s, k):
+        m = MA[k]
+        op("P", lambda: P.matmul(T.pc[:, 0:K - m], bdb, T.ov[:, m:K], True, True), part("ov", m, K) + ["bd"], ["pc"])
+
+    def count_a(s, k, opens=True):
+        pa, m = banks(s, k)[0], MA[k]
+        op("P", lambda: P.matmul(T[pa][:, 0:m], bdb, T.ov[:, 0:m], opens, not opens), part("ov", 0, m) + ["bd"], [pa])
+
+    def enough(s, k):
+        pb, m = banks(s, k)[1], MA[k]
+        op("A", lambda: S.activation(T.cr[:, m:K], T.pc[:, 0:K - m], Fn.Relu, bias=-UNIT), ["pc"], ["cr"])
+        op("P", lambda: P.matmul(T[pb][:, 0:K - m], bda, T.cr[:, m:K], True, False), ["cr", "bd"], [pb])
 
     def empty(s, k, opens=False):
         lst, lk, _h, _hk = arrival(s, k)
         pa, pb = banks(s, k)
-        op("A", lambda: S.activation(T.ab[:], win("bb", lst), Fn.Abs, scale=2.0 ** 64), ["bb", lk], ["ab"])
-        op("P", lambda: P.matmul(T[pb][:, 0:K - MA], T.bda[:], T.ab[:, MA:K], opens, not opens), ["ab", "bda"], [pb])
-        op("P", lambda: P.matmul(T[pa][:, 0:MA], T.bda[:], T.ab[:, 0:MA], opens, not opens), ["ab", "bda"], [pa])
+        m = MA[k]
+
+        def take(a, b):
+            op("A", lambda: S.activation(T.ab[:, a:b], win("bb", arrival(s, k, a, b)[0]), Fn.Abs, scale=2.0 ** 64),
+               ["bb", lk], part("ab", a, b))
+        take(m if k in SPLIT else 0, K)
+        if m < K:
+            op("P", lambda: P.matmul(T[pb][:, 0:K - m], bda, T.ab[:, m:K], False, True), part("ab", m, K) + ["bd"], [pb])
+        if k in SPLIT:
+            take(0, m)
+        if m:
+            op("P", lambda: P.matmul(T[pa][:, 0:m], bda, T.ab[:, 0:m], opens, not opens), part("ab", 0, m) + ["bd"], [pa])
 
     def make_sum(s, k):
         lst, lk, _h, _hk = arrival(s, k)
         gb = "g%d" % (k % 3)
-        op("V", lambda: V.tensor_tensor(T.sm[:], win("bb", lst), T[gb][:], A.add), ["bb", lk, gb], ["sm"])
+        op("V", lambda: V.tensor_tensor(T.sm[:], win("bb", lst), T[gb][:], A.add), ["bb", lk] + part(gb), ["sm"])
 
     def mask_b(s, k):
-        pb = banks(s, k)[1]
-        op("A", lambda: S.activation(T.mt[:], T[pb][:, 0:K - MA], Fn.Relu, bias=-THR), [pb], ["mt"])
-        op("A", lambda: S.activation(T.mk[:, MA:K], T.mt[:], Fn.Sign), ["mt"], ["mkB"])
+        pb, m = banks(s, k)[1], MA[k]
+        if m < K:
+            op("A", lambda: S.activation(T.mk[:, m:K], T[pb][:, 0:K - m], Fn.Sign), [pb], ["mkB"])
 
-    def put(s, k, both):
+    def put(s, k):
         lst, lk, _h, _hk = arrival(s, k)
-        pa, pb = banks(s, k)
-        if both:
-            op("V", lambda: V.tensor_scalar(T.mk[:, MA:K], T[pb][:, 0:K - MA], THR, None, A.is_gt), [pb], ["mkB"])
-        op("V", lambda: V.tensor_scalar(T.mk[:, 0:MA], T[pa][:, 0:MA], THR, None, A.is_gt), [pa], ["mkA"])
+        pa, m = banks(s, k)[0], MA[k]
+        if m:
+            op("V", lambda: V.tensor_scalar(T.mk[:, 0:m], T[pa][:, 0:m], UNIT, None, A.is_gt), [pa], ["mkA"])
+        if k in (1, 2) and EARLY[k - 1]:
+            far_list(s, k + 2)
+        if k in (1, 3):
+            c_scatter(s, k // 2)
         op("V", lambda: V.tensor_tensor(win("bb", lst), T.sm[:], T.mk[:], A.mult), ["sm", "mkA", "mkB", lk], ["bb"])
 
     def keys():
-        for k in range(3):
-            op("A", lambda k=k: S.activation(T.xk[:, k, :], T.pl[:, :, k], Fn.Identity, bias=float((2 - k) * W)),
-               ["pl"], ["xk"])
+        op("P", lambda: P.matmul(T.pv[:, 0:96], T.one[0:1, :], T.kc[0:1, :], True, False), ["one", "kc"], ["pv"])
+        for t in range(3):
+            sort_groups(lambda cp, t=t: T.pv[:, 3 * cp + t:96:6], t, t + 1, "pv", False)
+
+    def hold(s):
+        op("A", lambda: S.activation(win("held", T["e%d" % s][:]), T["sh%d" % s][:], Fn.Silu), ["sh%d" % s, "e%d" % s], ["held"])
 
     def election(s):
-        dn_, do_ = "d%d" % (s + 1), "d%d" % s
-        for hf in range(2):
-            a, b = hf * H, (hf + 1) * H
+        ek, en = "e%d" % s, "e%d" % (s + 1)
+        old, oldk = (T.d0[:], "d0") if s == 0 else (T.dn0[:, 2::3], "dn0")
+        mark, half = T["sh%d" % s], MARK[s] / 2.0
+        cols = ((0, EL), (EL, K))
+        for hf, (a, b) in enumerate(cols):
             for k in range(3):
-                lst = T.xl[:, 32 * k + 16 * hf:32 * k + 16 * hf + 16]
+                lst, lk, _h, _hk = arrival(s, k, a, b)
                 op("A", lambda k=k, lst=lst, a=a, b=b: S.activation(T.mm[:, k, a:b], win("bb", lst), Fn.Abs),
-                   ["bb", "x%d" % k], ["m%d%d" % (k, hf)])
-        op("A", lambda: S.activation(win("held", T.d16[:]), T["sh%d" % s][:], Fn.Silu), ["sh%d" % s, "d16"], ["held"])
+                   ["bb", lk], ["m%d%d" % (k, hf)])
 
         def max01(hf):
-            a, b = hf * H, (hf + 1) * H
+            a, b = cols[hf]
             op("V", lambda: V.tensor_tensor(T.pm[:, a:b], T.mm[:, 0, a:b], T.mm[:, 1, a:b], A.max),
-               ["m0%d" % hf, "m1%d" % hf], ["pm%d" % hf])
+               ["m0%d" % hf, "m1%d" % hf, "pm"], ["pm%d" % hf] + (["pm"] if hf == 0 else []))
 
         def max2(hf):
-            a, b = hf * H, (hf + 1) * H
+            a, b = cols[hf]
             op("V", lambda: V.tensor_tensor(T.pm[:, a:b], T.pm[:, a:b], T.mm[:, 2, a:b], A.max),
-               ["pm%d" % hf, "m2%d" % hf], ["pm%d" % hf])
+               ["pm%d" % hf, "m2%d" % hf, "pm"], ["pm%d" % hf])
 
         def vote(hf, k):
-            a, b = hf * H, (hf + 1) * H
-            op("V", lambda: V.tensor_tensor(T.vv[:, k, a:b], T.pm[:, a:b], T.mm[:, k, a:b], A.is_equal),
-               ["pm%d" % hf, "m%d%d" % (k, hf)], ["v%d%d" % (k, hf)])
+            a, b = cols[hf]
+            op("V", lambda: V.tensor_tensor(T.vv[:, a:b, k], T.pm[:, a:b], T.mm[:, k, a:b], A.is_equal),
+               ["pm%d" % hf, "m%d%d" % (k, hf), "pm"], ["v%d%d" % (k, hf)])
 
         def votes(hf):
-            a, b = hf * H, (hf + 1) * H
+            a, b = cols[hf]
 
             def fn():
                 last = None
                 for i in range(16):
-                    last = P.matmul(T.pv[:, 0:3, 16 * hf:16 * hf + 16], T.sel[:, 15 - i:143 - i], T.vv[:, :, a + i:b:16],
-                                    i == 0, i == 15)
+                    last = P.matmul(T.pv[:, 3 * a // 16:3 * b // 16], T.sel[:, 15 - i:143 - i], T.vv[:, a + i:b:16, :],
+                                    False, hf == 1 and i == 15)
                 return last
             op("P", fn, ["sel", "v0%d" % hf, "v1%d" % hf, "v2%d" % hf], ["pv"])
+        c_scatter(s, 3)
         max01(0)
+        op("V", lambda: V.tensor_copy(T.bs[:, 2::3], old), [oldk, "bs"], ["bs3"])
         max2(0)
         vote(0, 0)
         vote(0, 1)
@@ -340,78 +441,87 @@ def rank_program(g, core, T, topo):
         for k in range(3):
             vote(1, k)
         votes(1)
-        c_scatter(s, 3)
-        op("V", lambda: V.tensor_tensor(T.key[:], T.pv[:, 0:3, :], T.xk[:], A.add), ["pv", "xk"], ["key"])
-        op("V", lambda: V.tensor_tensor(T.k01[:], T.key[:, 0, :], T.key[:, 1, :], A.max), ["key"], ["k01"])
-        op("V", lambda: V.tensor_tensor(T.kk[:], T.k01[:], T.key[:, 2, :], A.max), ["key", "k01"], ["kk"])
-        op("V", lambda: V.tensor_scalar(T.lw[:, 0:32], T.kk[:], 4 * W - 1, None, A.bitwise_and), ["kk"], ["lwL"])
-        op("V", lambda: V.tensor_scalar(T.lw[:, 32:64], T.kk[:], W - 1, None, A.bitwise_and), ["kk"], ["lwW"])
+        c_scatter(s, 4)
+        op("V", lambda: V.tensor_tensor_scan(T.ks[:], T.pat[:], T.pv[:, 0:96], 0.0, A.mult, A.max), ["pv", "pat"], ["ks"])
+        op("P", lambda: P.matmul(T.pv[:, 96:192], T.one[0:1, :], T.pat[0:1, :], True, False), ["one", "pat"], ["pv"])
+        op("V", lambda: V.tensor_scalar(T.lw[:, 0:32], T.ks[:, 2::3], 4 * W - 1, None, A.bitwise_and), ["ks"], ["lwL"])
+        op("V", lambda: V.tensor_scalar(T.lw[:, 32:64], T.ks[:, 2::3], W - 1, None, A.bitwise_and), ["ks"], ["lwW"])
         op("V", lambda: V.tensor_copy(T.lw16[:], T.lw[:]), ["lwL", "lwW"], ["lw16"])
-        wish = T.lw16[:, 32:64]
-        op("V", lambda: V.tensor_copy(win("first", T.lw16[:, 0:32], 0, 3 * W), T["sf%d" % s][:]),
-           ["lw16", "sf%d" % s], ["first"])
-        op("A", lambda: S.activation(T.hg[:], win("held", wish), Fn.Copy, scale=0.125), ["held", "lw16"], ["hg"])
-        op("A", lambda: S.activation(T.lk[:, 0, :], win("first", wish, 2 * W, 3 * W), Fn.Copy, scale=2.0),
-           ["first", "lw16"], ["lkA"])
-        op("V", lambda: V.tensor_tensor(T.lk[:, 1, :], win("first", wish, W, 2 * W), T.hg[:], A.add),
-           ["first", "lw16", "hg"], ["lkB"])
+        op("A", lambda: S.activation(win("st", T.lw16[:, 0:32], 0, 3 * W), mark[:], Fn.Silu), ["lw16", "sh%d" % s], ["st"])
+        op("V", lambda: V.tensor_scalar(T.l1[:], T.lw[:, 0:32], 2 * W, None, A.min), ["lwL"], ["l1"])
+        op("V", lambda: V.tensor_scalar(T.l2[:], T.lw[:, 0:32], W, None, A.min), ["lwL"], ["l2"])
+        op("V", lambda: V.tensor_scalar(T.hg[:], win("held", T.lw16[:, 32:64]), half, half, A.is_le, A.mult),
+           ["held", "lw16"], ["hg"])
+        op("V", lambda: V.tensor_tensor(T.bs[:, 0::3], T.lw[:, 32:64], old, A.subtract), ["lwW", oldk, "bs"], ["bs0"])
+        c_scatter(s, 5)
+        op("A", lambda: S.activation(T.lk[:, :, 1], win("st", T.l1[:], W, 3 * W + 8), Fn.Relu, bias=-1.0, scale=1.0 / half),
+           ["st", "stz", "l1"], ["lkA"])
+        op("V", lambda: V.tensor_tensor(T.lk[:, :, 2], win("st", T.l2[:], 2 * W, 3 * W + 8), T.hg[:], A.is_ge),
+           ["st", "stz", "l2", "hg"], ["lkB"])
 
         def look():
             last = None
             for i in range(16):
-                last = P.matmul(T.pk[:, 0:2, :], T.sel[:, 15 - i:143 - i], T.lk[:, :, i::16], i == 0, i == 15)
+                last = P.matmul(T.pv[:, 96:192], T.seln[:, 15 - i:143 - i], T.lk[:, i::16, :], False, i == 15)
             return last
-        op("P", look, ["sel", "lkA", "lkB"], ["pk"])
-        u = 16.0 * SELW
-        al, be = ((1.5 * u / W, 0.25 * u), (24.0 * u / W, 8.0 * u))[s]
-        op("V", lambda: V.tensor_tensor(T.rr[:], T.lw[:, 0:32], T.lw[:, 32:64], A.subtract), ["lwL", "lwW"], ["rr"])
-        op("V", lambda: V.tensor_tensor(T.dif[:], T.lw[:, 32:64], T[do_][:], A.subtract), ["lwW", do_], ["dif"])
-        op("V", lambda: V.tensor_scalar(T.thr[:], T.rr[:], al, be, A.mult, A.add), ["rr"], ["thr"])
-        op("V", lambda: V.tensor_tensor(T.tt[:], T.thr[:], T.pk[:, 0, :], A.subtract), ["thr", "pk"], ["tt"])
-        op("V", lambda: V.tensor_tensor(T.go[:], T.pk[:, 1, :], T.tt[:], A.is_lt), ["tt", "pk"], ["go"])
-        op("V", lambda: V.tensor_tensor(T.dd[:], T.go[:], T.dif[:], A.mult), ["go", "dif"], ["dd"])
-        op("V", lambda: V.tensor_tensor(T[dn_][:], T.dd[:], T[do_][:], A.add), ["dd", do_], [dn_])
-        op("V", lambda: V.tensor_copy(T.d16[:], T[dn_][:]), [dn_], ["d16"])
+        op("P", look, ["seln", "lk0", "lkA", "lkB"], ["pv"])
+        c_scatter(s, 6)
+        dn = "dn%d" % s
+        op("V", lambda: V.tensor_tensor_scan(T[dn][:], T.pv[:, 96:192], T.bs[:], 0.0, A.mult, A.add),
+           ["pv", "bs", "bs0", "bs3"], [dn])
+        op("V", lambda: V.tensor_copy(T[en][:], T[dn][:, 2::3]), [dn], [en])
 
     for s in range(RO):
-        h = T["snd%d" % s][:, 0:K]
-        hk = "h%d" % s
-        if s == 0:
-            zero_b()
-            op("A", lambda: S.activation(T.nth[:, 0:1], T.ths[:, 0:1], Fn.Copy, scale=-1.0), ["ths"], ["nth"])
-            op("A", lambda: S.activation(T.bdb[:], T.bda[:], Fn.Copy, scale=2.0 ** -66), ["bda"], ["bdb"])
-            op("A", lambda: S.activation(T.sel[:, 15:128:16], T.bda[:, 15:128:16], Fn.Copy, scale=SELW * 2.0 ** -46),
-               ["bda", "sel"], ["sel"])
-            op("V", lambda: V.tensor_scalar(T.nb[:], win("b0s", T.d16[:]), -1.0, None, A.mult), ["b0s", "d16"], ["nb"])
-            op("V", lambda: V.tensor_tensor(T.dl[:], win("recs", T.d16[:]), T.nb[:], A.mult), ["recs", "d16", "nb"], ["dl"])
-            table_gather()
-        else:
-            op("A", lambda: S.activation(T.nb[:], win("bb", T.d16[:]), Fn.Copy, scale=-1.0), ["bb", "d16"], ["nb"])
-            zero_b()
-            c_gather(0, H)
-            table_gather()
-            op("V", lambda: V.tensor_tensor(T.dl[:], win("recs", T.d16[:]), T.nb[:], A.mult), ["recs", "d16", "nb"], ["dl"])
-        table_turn()
-        op("V", lambda h=h: V.tensor_tensor(h, win("ws", T.d16[:]), T.dl[:], A.mult), ["ws", "d16", "dl"], [hk])
-        lists_and_send(s)
-        if s == 0:
-            gfill(T.cc[:, 64:W], W - 64, 0, "cR")
-            gfill(T.held[:], W, 0, "held")
-            gfill(T.sh0[:], K, 32, "sh0")
-            gfill(T.sf0[:], K, 1, "sf0")
-            gfill(T.first[:, W:3 * W], 2 * W, 0, "first")
-            gfill(T.sh1[:], K, 512, "sh1")
-            gfill(T.sf1[:], K, 16, "sf1")
         last = s == RO - 1
-        empty(s, 0, True)
-        hop_list(1)
+        if s == 0:
+            zero_b(s)
+            take_b(s, 0, K)
+            delta(s, 0, K)
+            table_gather(s)
+            limit(0)
+            table_turn()
+            limit(1)
+            make_h(s, 0, K)
+            limit(2)
+        else:
+            take_b(s, 0, K)
+            zero_b(s)
+            table_gather(s)
+            delta(s, 0, K)
+            table_turn()
+            make_h(s, 0, K)
+        list0()
+        send(s)
+        if s == 0:
+            limit(3)
+            limit(4)
         make_g(s, 0)
+        if s == 0:
+            gfill(T.cc[:, 64:W], [[0, W - 64]], 0, ["cR"])
+            gfill(T.kc[:], [[0, 32], [-W, 3]], 2 * W, ["kc"])
+            gfill(T.one[:], [[0, 128]], 1, ["one"])
+            gfill(T.sel[:], [[0, 144]], int(SELW), ["sel"])
+            gfill(T.seln[:], [[0, 144]], -1, ["seln"])
+            gfill(T.pat[:], [[0, 96]], 1, ["pat"])
+            gkeep("sel", [[0, 9], [1, 16]], A.is_equal, -15, 0)
+            gkeep("seln", [[0, 9], [1, 16]], A.is_equal, -15, 0)
+            gkeep("pat", [[0, 32], [1, 3]], A.not_equal, 0, 0)
+            gkeep("sel", [[1, 144]], A.is_ge, 0, -1)
+            gkeep("seln", [[1, 144]], A.is_equal, -15, -1)
+            gkeep("sel", [[-1, 144]], A.is_ge, 15, 1)
+            gfill(T.bs[:], [[0, 96]], 0, ["bs"])
+            gfill(T.lk[:, :, 0], [[0, K]], 0, ["lk0"])
+            gfill(T.held[:], [[0, W]], 0, ["held"])
+            gfill(T.sh0[:], [[0, K]], MARK[0], ["sh0"])
+            gfill(T.st[:, W:3 * W + 8], [[0, 2 * W + 8]], 0, ["st", "stz"])
+            gfill(T.sh1[:], [[0, K]], MARK[1], ["sh1"])
+        empty(s, 0, True)
         size(0)
-        over(s, 0, False)
+        list12()
         make_g(s, 1)
-        hop_list(2)
+        over()
+        count_a(s, 0, False)
         make_sum(s, 0)
-        c_scatter(s, 0)
         for k in range(5):
             if k > 0:
                 empty(s, k)
@@ -419,22 +529,33 @@ def rank_program(g, core, T, topo):
                     make_g(s, k + 1)
                 make_sum(s, k)
             if k < 4:
-                size(k + 1)
-                mask_b(s, k)
-            elif last:
-                c_scatter(s, 1)
-                op("S", lambda: Y.dma_start(T.yc[:], T.cc[:]).then_inc(T.sem.o_c, 16), C2, ["yc"], ("o_c", 16))
+                size(k + 1, SQ if k else 0, K)
             else:
-                c_scatter(s, 1)
-            put(s, k, k == 4)
+                c_scatter(s, 2)
+                if last:
+                    op("S", lambda: Y.dma_start(T.yc[:], T.cc[:]).then_inc(T.sem.o_c, 16), C2, ["yc"], ("o_c", 16))
+            mask_b(s, k)
+            put(s, k)
             if k < 4:
-                over(s, k + 1)
-            if k == 0 and not last:
+                m = MA[k + 1]
+                if k and SQ:
+                    size(k + 1, 0, SQ)
+                if MODE:
+                    over(m, K)
+                    count_b(s, k + 1)
+                    over(0, m)
+                else:
+                    over()
+                    count_b(s, k + 1)
+                count_a(s, k + 1)
+                if s > 0 and k in CG:
+                    c_gather(s, *CG[k])
+                enough(s, k + 1)
+            if k == 3 and not last:
                 keys()
-            if k == 1 and s > 0:
-                c_gather(H, K)
+            if k == 4 and not last:
+                hold(s)
         if not last:
-            c_scatter(s, 2)
             election(s)
 
     op("S", lambda: Y.dma_start(T.yb[:], T.bb[:]).then_inc(T.sem.o_b, 16), ["bb"], ["yb"], ("o_b", 16))

@@ -4,51 +4,42 @@ W, K, RO = 2048, 512, 3
 F32, BF, F16, I32, U16 = "float32", "bfloat16", "float16", "int32", "uint16"
 MSG = K + 64
 H = K // 2
-MA = [512, 256, 256, 256, 192]
-CUTS = [[0, 0, 0, 64, 160, 256, 416, 512], [0, 0, 0, 64, 160, 256, 416, 512], [0, 128, 256, 512]]
-SLA = True
-SPLIT = [4]
-MODE = 1
-SQ = 0
-CG = {0: (0, 256), 1: (256, 512)}
-EARLY = [0, 1, 0]
-EL = 192
-TBV = 1536
-CPG = 0
-ROW0, ROWS = 0, 3
+MA = [256, 128, 128, 128, 192]
+CUTS = [[0, 0, 0, 64, 192, 256, 384, 512], [0, 0, 0, 64, 192, 256, 384, 512], [0, 128, 256, 512]]
+TBV = 1360
+ROWS = 3
 UNIT = 2.0 ** -20
+BIG = 384
 TOP = 2.0 - 2.0 ** -13
-SELW = 8192.0
-X0 = 448
+SELW = 8192
 MARK = (32, 512)
 
 SCRATCH = {
-    "bb": ("sbuf", [128, W], F32), "cc": ("sbuf", [128, W], F32), "held": ("sbuf", [128, W], F32),
-    "tb": ("sbuf", [128, W], I32), "st": ("sbuf", [128, 3 * W + 8], F32),
+    "bb": ("sbuf", [128, W], F32), "cc": ("sbuf", [128, W], F32),
+    "tb": ("sbuf", [128, W], I32), "st": ("sbuf", [128, 4 * W + 8], F32),
     "b0s": ("sbuf", [128, W], BF), "ws": ("sbuf", [128, W], BF), "recs": ("sbuf", [128, W], BF),
-    "ths": ("sbuf", [128, 8], F32), "aux": ("sbuf", [128, 8], F32), "rough": ("sbuf", [128, 16], BF),
-    "sc": ("sbuf", [128, 8], F32), "lim": ("sbuf", [128, 8], F32),
+    "row": ("sbuf", [128, 128], F32), "ths": ("sbuf", [128, 8], F32), "aux": ("sbuf", [128, 8], F32),
+    "rough": ("sbuf", [128, 16], BF), "sc": ("sbuf", [128, 8], F32), "lim": ("sbuf", [128, 8], F32),
     "zin": ("sbuf", [128, K], F32), "sh0": ("sbuf", [128, K], F32), "sh1": ("sbuf", [128, K], F32),
     "ones": ("sbuf", [128, 160], F32), "jj": ("sbuf", [128, 160], F32),
     "pe": ("sbuf", [128, 160], F16), "po": ("sbuf", [128, 160], F16),
     "bd0": ("sbuf", [128, 2, 128], BF), "bd1": ("sbuf", [128, 2, 128], BF), "bd": ("sbuf", [128, 2, 128], BF),
     "sel": ("sbuf", [128, 144], BF), "seln": ("sbuf", [128, 144], BF),
-    "one": ("sbuf", [128, 128], BF), "kc": ("sbuf", [128, 96], BF), "pat": ("sbuf", [128, 96], BF),
+    "one": ("sbuf", [128, 128], BF), "cst": ("sbuf", [128, 2, K], BF), "kc": ("sbuf", [128, 96], BF),
+    "pat": ("sbuf", [128, 96], BF), "pat4": ("sbuf", [128, 128], BF),
     "d0": ("sbuf", [128, 32], I32), "e0": ("sbuf", [128, 32], U16), "e1": ("sbuf", [128, 32], U16),
     "e2": ("sbuf", [128, 32], U16),
-    "x0": ("sbuf", [128, 32], U16), "x12": ("sbuf", [128, 64], U16), "xu": ("sbuf", [128, 32], U16),
-    "xd": ("sbuf", [128, 32], U16), "lw16": ("sbuf", [128, 64], U16), "l1": ("sbuf", [128, 32], U16),
-    "l2": ("sbuf", [128, 32], U16),
+    "xl": ("sbuf", [128, 96], U16), "xu": ("sbuf", [128, 32], U16), "xd": ("sbuf", [128, 32], U16),
+    "l1": ("sbuf", [128, 32], U16), "l2": ("sbuf", [128, 32], U16),
     "nb": ("sbuf", [128, K], F32), "dl": ("sbuf", [128, K], F32), "cd": ("sbuf", [128, K], F32),
     "tg": ("sbuf", [128, K], F16), "tr": ("sbuf", [128, 16, 2, 16], F16),
     "g0": ("sbuf", [128, K], F32), "g1": ("sbuf", [128, K], F32), "g2": ("sbuf", [128, K], F32),
-    "sm": ("sbuf", [128, K], F32), "mk": ("sbuf", [128, K], F32), "cr": ("sbuf", [128, K], BF),
-    "ag": ("sbuf", [128, K], F32), "rl": ("sbuf", [128, K], F32), "ov": ("sbuf", [128, K], BF),
-    "ab": ("sbuf", [128, K], BF),
+    "sm": ("sbuf", [128, K], F32), "mk": ("sbuf", [128, K], F32),
+    "sq": ("sbuf", [128, K], F32), "ov": ("sbuf", [128, K], BF), "ab": ("sbuf", [128, K], BF),
     "mm": ("sbuf", [128, 3, K], F32), "vv": ("sbuf", [128, K, 3], BF),
-    "ks": ("sbuf", [128, 96], I32), "lw": ("sbuf", [128, 64], I32),
-    "bs": ("sbuf", [128, 96], F32), "dn0": ("sbuf", [128, 96], F32), "dn1": ("sbuf", [128, 96], F32),
-    "hg": ("sbuf", [128, K], BF), "lk": ("sbuf", [128, K, 3], BF),
+    "ks": ("sbuf", [128, 96], I32), "lw": ("sbuf", [128, 32], I32), "wish": ("sbuf", [128, 32], I32),
+    "bs": ("sbuf", [128, 128], F32), "dn0": ("sbuf", [128, 128], F32), "dn1": ("sbuf", [128, 128], F32),
+    "lk": ("sbuf", [128, K, 2], BF),
     "pa0": ("psum", [128, K], F32), "pb0": ("psum", [128, K], F32),
     "pa1": ("psum", [128, K], F32), "pb1": ("psum", [128, K], F32),
     "pc": ("psum", [128, K], F32), "pm": ("psum", [128, K], F32),
@@ -58,8 +49,10 @@ for _s in range(RO):
     for _n in ("snd", "lu", "lr", "ld"):
         SCRATCH["%s%d" % (_n, _s)] = ("sbuf", [128, MSG], F32)
 PSUM = ("pa0", "pb0", "pa1", "pb1", "pc", "pl", "pm", "pv")
+KEYS = ("pv", "pc")
+TOPS = ("pm", "pb0")
 
-SEMAPHORES = ["cV", "cA", "cP", "cG", "l_wk", "l_th", "l_b0", "l_rec", "l_w", "l_tb", "sent", "o_c", "o_b"]
+SEMAPHORES = ["cV", "cA", "cP", "cG", "l_wk", "l_th", "l_b0", "l_rec", "l_w", "l_tb", "sent", "o_c", "o_b", "hd0", "hd1"]
 for _s in range(RO):
     SEMAPHORES += ["au%d" % _s, "ad%d" % _s, "rot%d" % _s]
 
@@ -143,8 +136,8 @@ def rank_program(g, core, T, topo):
     A, Fn = AluOpType, ActivationFunctionType
     V, S, P, Y = g.vector, g.scalar, g.tensor, g.sync
     plan = new_plan()
-    C2 = ["cL", "cR"]
-    BB = ["bb", "bbG"]
+    C2, TB = ["cL", "cR"], ["tbL", "tbR"]
+    bda, bdb = T.bd[:, 0, :], T.bd[:, 1, :]
 
     def op(q, fn, reads=(), writes=(), dma=None):
         return add(plan, q, fn, reads, writes, dma)
@@ -158,85 +151,100 @@ def rank_program(g, core, T, topo):
     def load(q, eng, dst, src, sem, key):
         op(q, lambda: eng.dma_start(dst, src).then_inc(T.sem[sem], 16), [], [key], (sem, 16))
 
+    def gfill(ap, pattern, val, keys):
+        op("G", lambda: g.iota(ap, pattern, val, 0, allow_small_or_imprecise_dtypes=True), [], keys)
+
+    def gkeep(dst, src, pattern, test, base, mult, keys=None):
+        op("G", lambda: g.affine_select(T[dst][:], T[src][:], pattern, test, 0.0, base, mult), keys or [src], [dst])
+
     load("A", S, T.b0s[:], T.b0[:], "l_b0", "b0s")
     load("S", Y, T.d0[:], T.wk[:], "l_wk", "d0")
+    load("S", Y, T.row[0:1, :], T.th[:], "l_th", "row")
     load("S", Y, T.recs[:], T.rec[:], "l_rec", "recs")
-    load("S", Y, T.ws[:], T.w[:], "l_w", "ws")
-    TB = ["tbL", "tbR"]
     op("V", lambda: V.memset(T.zin[:, 0:64], -128.0), [], ["zin0"])
     op("V", lambda: V.memset(T.tb[:, 0:TBV], 0), [], ["tbL"])
     op("V", lambda: V.memset(T.ones[:], 1.0), [], ["ones"])
-    op("G", lambda: g.dma_start(T.ths[:, 0:1], T.th[:], allow_slow_non_contiguous=True).then_inc(T.sem.l_th, 16),
-       [], ["ths"], ("l_th", 16))
     op("G", lambda: g.iota(T.tb[:, TBV:W], [[0, W - TBV]], 0, 0), [], ["tbR"])
     op("V", lambda: V.memset(T.bd0[:, 0, :], 2.0 ** 46), [], ["bd0a"])
     op("V", lambda: V.memset(T.bd0[:, 1, :], UNIT), [], ["bd0b"])
-    bda, bdb = T.bd[:, 0, :], T.bd[:, 1, :]
-    op("V", lambda: V.memset(T.zin[:, 64:K], -128.0), [], ["zin"])
+    op("P", lambda: P.transpose(T.pa0[:, 0:1], T.row[0:1, :], T.ones[0:1, 0:1]), ["row", "ones"], ["pa0"])
 
     def tables():
         for t in range(5):
             src = T.hop[:, t * W:(t + 1) * W] if t < 3 else (T.up[:] if t == 3 else T.dn[:])
-            Y.dma_start(T.tb[ROW0 + ROWS * t::16, :], src).then_inc(T.sem.l_tb, 16)
+            Y.dma_start(T.tb[ROWS * t::16, :], src).then_inc(T.sem.l_tb, 16)
     op("S", tables, [], TB, ("l_tb", 80))
+    load("S", Y, T.ws[:], T.w[:], "l_w", "ws")
 
-    op("G", lambda: g.affine_select(T.jj[:], T.ones[:], [[1, 160]], A.is_equal, 0.0, -16, -1), ["ones"], ["jj"])
-    op("G", lambda: g.affine_select(T.bd1[:], T.bd0[:], [[0, 2], [-16, 8], [0, 16]], A.is_ge, 0.0, 0, 1),
-       ["bd0a", "bd0b"], ["bd1"])
-    op("G", lambda: g.affine_select(T.pe[:], T.jj[:], [[0, 5], [1, 2], [0, 16]], A.is_gt, 0.0, 0, 0), ["jj"], ["pe"])
-    op("G", lambda: g.affine_select(T.po[:], T.jj[:], [[0, 5], [1, 2], [0, 16]], A.is_equal, 0.0, 0, 0), ["jj"], ["po"])
-    if CPG:
-        op("G", lambda: g.affine_select(T.bb[:, W - CPG:W], T.b0s[:, W - CPG:W], [[0, CPG]], A.is_equal, 0.0, 0, 0),
-           ["b0s"], ["bbG"])
-    op("G", lambda: g.affine_select(T.bd[:], T.bd1[:], [[0, 2], [16, 8], [0, 16]], A.is_ge, 0.0, 15, -1), ["bd1"], ["bd"])
-
-    def gfill(ap, pattern, val, keys):
-        op("G", lambda: g.iota(ap, pattern, val, 0, allow_small_or_imprecise_dtypes=True), [], keys)
-
-    def gkeep(name, pattern, test, base, mult):
-        op("G", lambda: g.affine_select(T[name][:], T[name][:], pattern, test, 0.0, base, mult), [name], [name])
+    gkeep("jj", "ones", [[1, 160]], A.is_equal, -16, -1)
+    gkeep("bd1", "bd0", [[0, 2], [-16, 8], [0, 16]], A.is_ge, 0, 1, ["bd0a", "bd0b"])
+    gkeep("pe", "jj", [[0, 5], [1, 2], [0, 16]], A.is_gt, 0, 0)
+    gkeep("po", "jj", [[0, 5], [1, 2], [0, 16]], A.is_equal, 0, 0)
+    gkeep("bd", "bd1", [[0, 2], [16, 8], [0, 16]], A.is_ge, 15, -1)
+    gfill(T.one[0:1, :], [[0, 128]], 1, ["one"])
+    for i, v in enumerate((15, BIG)):
+        gfill(T.cst[0:1, i, min(MA):K], [[0, K - min(MA)]], v, ["cst%d" % i])
     op("A", lambda: S.activation(T.cc[:, 0:64], T.zin[:, 0:64], Fn.Silu), ["zin0"], ["cL"])
-    op("A", lambda: S.activation(T.bb[:, 0:W - CPG], T.b0s[:, 0:W - CPG], Fn.Copy), ["b0s"], ["bb"])
+    ZIN = range(64, K, 160)
+    for a in ZIN:
+        op("A", lambda a=a: S.activation(T.zin[:, a:min(a + 160, K)], T.ones[:, 0:min(160, K - a)], Fn.Copy, scale=-128.0),
+           ["ones"], ["zin%d" % a])
+    op("A", lambda: S.activation(T.bb[:], T.b0s[:], Fn.Copy), ["b0s"], ["bb"])
     op("V", lambda: V.tensor_copy(T.e0[:], T.d0[:]), ["d0"], ["e0"])
 
     def limit(i):
         th, c = T.ths[:, 0:1], lambda j: T.aux[:, j:j + 1]
         if i == 0:
-            op("V", lambda: V.reciprocal(c(0), th), ["ths"], ["aux0"])
-        if i == 1:
+            op("V", lambda: V.reciprocal(c(0), T.pa0[:, 0:1]), ["pa0"], ["aux0"])
+            op("V", lambda: V.tensor_copy(th, T.pa0[:, 0:1]), ["pa0"], ["ths"])
             op("V", lambda: V.tensor_scalar(T.rough[:, 0:1], c(0), TOP, None, A.mult), ["aux0"], ["rough"])
             op("V", lambda: V.tensor_scalar(c(1), c(0), TOP, None, A.mult), ["aux0"], ["aux1"])
-        if i == 2:
+        if i == 1:
             op("V", lambda: V.tensor_scalar(c(2), th, T.rough[:, 0:1], 2.0, A.mult, A.is_lt), ["ths", "rough"], ["aux2"])
-        if i == 3:
+        if i == 2:
             op("V", lambda: V.tensor_scalar(T.sc[:, 0:1], T.rough[:, 0:1], c(2), c(1), A.mult, A.max),
                ["aux1", "aux2", "rough"], ["sc"])
-        if i == 4:
+        if i == 3:
             op("A", lambda: S.activation(c(3), th, Fn.Square, scale=T.sc[:, 0:1]), ["ths", "sc"], ["aux3"])
             op("A", lambda: S.activation(T.lim[:, 0:1], c(3), Fn.Identity, bias=-2.0 ** -22, scale=-1.0), ["aux3"], ["lim"])
 
-    def take_b(s, a, b):
-        e = T["e%d" % s][:, a // 16:b // 16]
+    def later_constants():
+        gfill(T.cc[:, 64:W], [[0, W - 64]], 0, ["cR"])
+        gfill(T.kc[:], [[0, 32], [-W, 3]], 2 * W, ["kc"])
+        gfill(T.st[:, 2 * W:4 * W + 8], [[0, 2 * W + 8]], 0, ["held", "st"])
+        gfill(T.sh0[:], [[0, K]], MARK[0], ["sh0"])
+        gfill(T.sel[:], [[0, 144]], SELW, ["sel"])
+        gfill(T.seln[:], [[0, 144]], -1, ["seln"])
+        gfill(T.pat[:], [[0, 96]], 1, ["pat"])
+        gkeep("sel", "sel", [[0, 9], [1, 16]], A.is_equal, -15, 0)
+        gkeep("seln", "seln", [[0, 9], [1, 16]], A.is_equal, -15, 0)
+        gkeep("pat", "pat", [[0, 32], [1, 3]], A.not_equal, 0, 0)
+        gkeep("sel", "sel", [[1, 144]], A.is_ge, 0, -1)
+        gkeep("seln", "seln", [[1, 144]], A.is_equal, -15, -1)
+        gkeep("sel", "sel", [[-1, 144]], A.is_ge, 15, 1)
+        gfill(T.bs[:], [[0, 128]], 0, ["bs"])
+        gfill(T.pat4[:], [[0, 128]], 1, ["pat4"])
+        gkeep("pat4", "pat4", [[0, 32], [1, 4]], A.not_equal, 0, 0)
+        gfill(T.st[:, W:2 * W], [[0, W]], 0, ["st1"])
+        gfill(T.sh1[:], [[0, K]], MARK[1], ["sh1"])
+
+    def take_b(s):
+        ek = "e%d" % s
         if s == 0:
-            op("V", lambda: V.tensor_scalar(T.nb[:, a:b], win("b0s", e), -1.0, None, A.mult), ["b0s", "e0"], part("nb", a, b))
+            op("V", lambda: V.tensor_scalar(T.nb[:], win("b0s", T[ek][:]), -1.0, None, A.mult), ["b0s", ek], ["nb"])
         else:
-            op("A", lambda: S.activation(T.nb[:, a:b], win("bb", e), Fn.Copy, scale=-1.0), ["bb", "e%d" % s], part("nb", a, b))
+            op("A", lambda: S.activation(T.nb[:], win("bb", T[ek][:]), Fn.Copy, scale=-1.0), ["bb", ek], ["nb"])
 
     def zero_b(s):
-        op("A", lambda: S.activation(win("bb", T["e%d" % s][:]), T.zin[:], Fn.Silu), ["zin0", "zin", "e%d" % s], BB)
+        op("A", lambda: S.activation(win("bb", T["e%d" % s][:]), T.zin[:], Fn.Silu),
+           ["zin0", "e%d" % s] + ["zin%d" % a for a in ZIN], ["bb"])
 
-    def delta(s, a, b):
-        e = T["e%d" % s][:, a // 16:b // 16]
-        op("V", lambda: V.tensor_tensor(T.dl[:, a:b], win("recs", e), T.nb[:, a:b], A.mult),
-           ["recs", "e%d" % s] + part("nb", a, b), part("dl", a, b))
+    def delta(s):
+        op("V", lambda: V.tensor_tensor(T.dl[:], win("recs", T["e%d" % s][:]), T.nb[:], A.mult), ["recs", "e%d" % s, "nb"], ["dl"])
 
-    def make_h(s, a, b):
-        e = T["e%d" % s][:, a // 16:b // 16]
-        op("V", lambda: V.tensor_tensor(T["snd%d" % s][:, a:b], win("ws", e), T.dl[:, a:b], A.mult),
-           ["ws", "e%d" % s] + part("dl", a, b), part("h%d" % s, a, b))
-
-    def table_gather(s):
-        op("V", lambda: V.tensor_copy(T.tg[:], win("tb", T["e%d" % s][:])), TB + ["e%d" % s], ["tg"])
+    def make_h(s):
+        op("V", lambda: V.tensor_tensor(T["snd%d" % s][:, 0:K], win("ws", T["e%d" % s][:]), T.dl[:], A.mult),
+           ["ws", "e%d" % s, "dl"], ["h%d" % s])
 
     def sort_groups(out, t0, t1, key, opens=True):
         def fn():
@@ -245,37 +253,30 @@ def rank_program(g, core, T, topo):
                 m = T.pe if cp == 0 else T.po
                 for gp in range(2):
                     a = 16 - 16 * (gp - cp)
-                    r0 = ROW0 + ROWS * t0
-                    rhs = T.tr[:, :, gp, r0] if t1 == t0 + 1 else T.tr[:, :, gp, r0:r0 + (t1 - t0 - 1) * ROWS + 1:ROWS]
+                    rhs = T.tr[:, :, gp, ROWS * t0:ROWS * (t1 - 1) + 1:ROWS]
                     last = P.matmul(out(cp), m[:, a:a + 128], rhs, opens and gp == 0, opens and gp == 1)
             return last
         op("P", fn, ["tr", "pe", "po"], [key])
 
-    def table_turn():
+    def table_lists(s):
+        op("V", lambda: V.tensor_copy(T.tg[:], win("tb", T["e%d" % s][:])), TB + ["e%d" % s], ["tg"])
         op("V", lambda: V.transpose(T.tr[:], T.tg[:]), ["tg"], ["tr"])
-        sort_groups(lambda cp: T.pc[:, X0 + cp:X0 + 32:2], 0, 1, "pc")
+        for t in range(3):
+            sort_groups(lambda cp, t=t: T.pm[:, 32 * t + cp:32 * t + 32:2], t, t + 1, "pm")
         sort_groups(lambda cp: T.pl[:, cp:32:2, :], 3, 5, "pl")
-        for t in (1, 2):
-            sort_groups(lambda cp, t=t: T.pm[:, 32 * t - 32 + cp:32 * t:2], t, t + 1, "pm")
 
-    def list0():
-        op("V", lambda: V.tensor_copy(T.x0[:], T.pc[:, X0:X0 + 32]), ["pc"], ["x0"])
-
-    def list12():
-        op("V", lambda: V.tensor_copy(T.x12[:], T.pm[:, 0:64]), ["pm"], ["x12"])
+    def hop_lists():
+        op("V", lambda: V.tensor_copy(T.xl[:], T.pm[:, 0:96]), ["pm"], ["xl"])
 
     def send(s):
         snd = T["snd%d" % s]
-        if SLA:
-            op("A", lambda: S.activation(snd[:, K:MSG], T.pl[:, 0:32, :], Fn.Copy), ["pl"], ["sl%d" % s])
-        else:
-            op("V", lambda: V.tensor_copy(snd[:, K:MSG], T.pl[:, 0:32, :]), ["pl"], ["sl%d" % s])
+        op("V", lambda: V.tensor_copy(snd[:, K:MSG], T.pl[:, 0:32, :]), ["pl"], ["sl%d" % s])
         for dst, land, sem in ((T.cores[(rank + 1) % n], "lu", "au"), (T.cores[(rank - 1) % n], "ld", "ad")):
             def write(dst=dst, land=land, sem=sem):
                 rid, pid, _e = topo.addr(dst)
                 g.remote_dma(T["%s%d" % (land, s)][:], snd[:], T.sem["%s%d" % (sem, s)], T.sem.sent, pid, rid,
                              topo.mask(core, dst))
-            op("G", write, part("h%d" % s) + ["sl%d" % s], [], ("sent", 0))
+            op("G", write, ["h%d" % s, "sl%d" % s], [], ("sent", 0))
         op(None, None, [], ["lu%d" % s], ("au%d" % s, len(topo.engines(T.cores[(rank - 1) % n], core))))
         op(None, None, [], ["ld%d" % s], ("ad%d" % s, len(topo.engines(T.cores[(rank + 1) % n], core))))
 
@@ -290,10 +291,10 @@ def rank_program(g, core, T, topo):
         a, b = CUTS[s][i], CUTS[s][i + 1]
         lst, ek = T["e%d" % s][:, a // 16:b // 16], "e%d" % s
         if s == 0:
-            op("V", lambda: V.tensor_copy(win("cc", lst), T.dl[:, a:b]), part("dl", a, b) + [ek], C2)
+            op("V", lambda: V.tensor_copy(win("cc", lst), T.dl[:, a:b]), ["dl", ek], C2)
         else:
             op("V", lambda: V.tensor_tensor(win("cc", lst), T.cd[:, a:b], T.dl[:, a:b], A.add),
-               part("dl", a, b) + part("cd", a, b) + [ek], C2)
+               ["dl", ek] + part("cd", a, b), C2)
 
     def c_gather(s, a, b):
         op("A", lambda: S.activation(T.cd[:, a:b], win("cc", T["e%d" % s][:, a // 16:b // 16]), Fn.Copy),
@@ -302,66 +303,60 @@ def rank_program(g, core, T, topo):
     def arrival(s, k, a=0, b=K):
         a16, b16 = a // 16, b // 16
         if k < 3:
-            lst = T.x0[:, a16:b16] if k == 0 else T.x12[:, 32 * k - 32 + a16:32 * k - 32 + b16]
-            return lst, "x0" if k == 0 else "x12", T["snd%d" % s][:, a:b], part("h%d" % s, a, b)
+            return T.xl[:, 32 * k + a16:32 * k + b16], "xl", T["snd%d" % s][:, a:b], "h%d" % s
         if k == 3:
-            return T.xu[:, a16:b16], "xu", T["lr%d" % s][:, a:b], ["lr%d" % s]
-        return T.xd[:, a16:b16], "xd", T["ld%d" % s][:, a:b], ["ld%d" % s]
+            return T.xu[:, a16:b16], "xu", T["lr%d" % s][:, a:b], "lr%d" % s
+        return T.xd[:, a16:b16], "xd", T["ld%d" % s][:, a:b], "ld%d" % s
 
     def far_list(s, k):
-        if k == 3:
-            op("V", lambda: V.tensor_copy(T.xu[:], T["lr%d" % s][:, K:MSG:2]), ["lr%d" % s], ["xu"])
-        if k == 4:
-            op("V", lambda: V.tensor_copy(T.xd[:], T["ld%d" % s][:, K + 1:MSG:2]), ["ld%d" % s], ["xd"])
+        _l, lk, _h, hk = arrival(s, k)
+        op("V", lambda: V.tensor_copy(T[lk][:], T[hk][:, K + k - 3:MSG:2]), [hk], [lk])
 
     def make_g(s, k, a=0, b=K):
         lst, lk, h, hk = arrival(s, k, a, b)
-        if k + 1 - EARLY[k - 3] == k + 1:
-            far_list(s, k)
         gb = "g%d" % (k % 3)
-        op("V", lambda: V.tensor_tensor(T[gb][:, a:b], win("ws", lst), h, A.mult), ["ws", lk] + hk, part(gb, a, b))
+        op("V", lambda: V.tensor_tensor(T[gb][:, a:b], win("ws", lst), h, A.mult), ["ws", lk, hk], part(gb, a, b))
 
     def banks(s, k):
         par = (5 * s + k) % 2
         return "pa%d" % par, "pb%d" % par
 
-    def size(k, a=0, b=K):
+    def square(k, a=0, b=K):
         gb = "g%d" % (k % 3)
-        op("A", lambda: S.activation(T.ag[:, a:b], T[gb][:, a:b], Fn.Square, scale=T.sc[:, 0:1]),
-           part(gb, a, b) + ["sc"], part("ag", a, b))
+        op("A", lambda: S.activation(T.sq[:, a:b], T[gb][:, a:b], Fn.Square, scale=T.sc[:, 0:1]),
+           part(gb, a, b) + ["sc"], part("sq", a, b))
 
     def over(a=0, b=K):
-        op("A", lambda: S.activation(T.ov[:, a:b], T.ag[:, a:b], Fn.Sign, bias=T.lim[:, 0:1]),
-           part("ag", a, b) + ["lim"], part("ov", a, b))
+        op("A", lambda: S.activation(T.ov[:, a:b], T.sq[:, a:b], Fn.Sign, bias=T.lim[:, 0:1]),
+           part("sq", a, b) + ["lim"], part("ov", a, b))
+
+    def size_b(s, k, a, b):
+        lst, lk, _h, _hk = arrival(s, k, a, b)
+        op("A", lambda: S.activation(T.ab[:, a:b], win("bb", lst), Fn.Abs, scale=2.0 ** 64), ["bb", lk], part("ab", a, b))
+
+    def offset(s, k):
+        pb, m = banks(s, k)[1], MA[k]
+        op("P", lambda: P.matmul(T[pb][:, 0:K - m], T.bd0[0:1, 1, :], T.cst[0:1, 0, m:K], True, False), ["bd0b", "cst0"], [pb])
 
     def count_b(s, k):
-        m = MA[k]
-        op("P", lambda: P.matmul(T.pc[:, 0:K - m], bdb, T.ov[:, m:K], True, True), part("ov", m, K) + ["bd"], ["pc"])
-
-    def count_a(s, k, opens=True):
-        pa, m = banks(s, k)[0], MA[k]
-        op("P", lambda: P.matmul(T[pa][:, 0:m], bdb, T.ov[:, 0:m], opens, not opens), part("ov", 0, m) + ["bd"], [pa])
-
-    def enough(s, k):
         pb, m = banks(s, k)[1], MA[k]
-        op("A", lambda: S.activation(T.cr[:, m:K], T.pc[:, 0:K - m], Fn.Relu, bias=-UNIT), ["pc"], ["cr"])
-        op("P", lambda: P.matmul(T[pb][:, 0:K - m], bda, T.cr[:, m:K], True, False), ["cr", "bd"], [pb])
 
-    def empty(s, k, opens=False):
-        lst, lk, _h, _hk = arrival(s, k)
-        pa, pb = banks(s, k)
-        m = MA[k]
+        def fn():
+            P.matmul(T[pb][:, 0:K - m], bdb, T.ov[:, m:K], False, False)
+            return P.matmul(T[pb][:, 0:K - m], T.one[0:1, :], T.cst[0:1, 1, m:K], False, k == 0)
+        op("P", fn, part("ov", m, K) + ["bd", "one", "cst1"], [pb])
 
-        def take(a, b):
-            op("A", lambda: S.activation(T.ab[:, a:b], win("bb", arrival(s, k, a, b)[0]), Fn.Abs, scale=2.0 ** 64),
-               ["bb", lk], part("ab", a, b))
-        take(m if k in SPLIT else 0, K)
-        if m < K:
-            op("P", lambda: P.matmul(T[pb][:, 0:K - m], bda, T.ab[:, m:K], False, True), part("ab", m, K) + ["bd"], [pb])
-        if k in SPLIT:
-            take(0, m)
-        if m:
-            op("P", lambda: P.matmul(T[pa][:, 0:m], bda, T.ab[:, 0:m], opens, not opens), part("ab", 0, m) + ["bd"], [pa])
+    def count_a(s, k):
+        pa, m = banks(s, k)[0], MA[k]
+        op("P", lambda: P.matmul(T[pa][:, 0:m], bdb, T.ov[:, 0:m], k > 0, k == 0), part("ov", 0, m) + ["bd"], [pa])
+
+    def empty_b(s, k):
+        pb, m = banks(s, k)[1], MA[k]
+        op("P", lambda: P.matmul(T[pb][:, 0:K - m], bda, T.ab[:, m:K], False, k > 0), part("ab", m, K) + ["bd"], [pb])
+
+    def empty_a(s, k):
+        pa, m = banks(s, k)[0], MA[k]
+        op("P", lambda: P.matmul(T[pa][:, 0:m], bda, T.ab[:, 0:m], k == 0, k > 0), part("ab", 0, m) + ["bd"], [pa])
 
     def make_sum(s, k):
         lst, lk, _h, _hk = arrival(s, k)
@@ -370,192 +365,205 @@ def rank_program(g, core, T, topo):
 
     def mask_b(s, k):
         pb, m = banks(s, k)[1], MA[k]
-        if m < K:
-            op("A", lambda: S.activation(T.mk[:, m:K], T[pb][:, 0:K - m], Fn.Sign), [pb], ["mkB"])
+        op("A", lambda: S.activation(T.mk[:, m:K], T[pb][:, 0:K - m], Fn.Sign, bias=-float(BIG)), [pb], ["mkB"])
 
     def put(s, k):
         lst, lk, _h, _hk = arrival(s, k)
         pa, m = banks(s, k)[0], MA[k]
-        if m:
-            op("V", lambda: V.tensor_scalar(T.mk[:, 0:m], T[pa][:, 0:m], UNIT, None, A.is_gt), [pa], ["mkA"])
-        if k in (1, 2) and EARLY[k - 1]:
-            far_list(s, k + 2)
+        op("V", lambda: V.tensor_scalar(T.mk[:, 0:m], T[pa][:, 0:m], UNIT, None, A.is_gt), [pa], ["mkA"])
         if k in (1, 3):
             c_scatter(s, k // 2)
         op("V", lambda: V.tensor_tensor(win("bb", lst), T.sm[:], T.mk[:], A.mult), ["sm", "mkA", "mkB", lk], ["bb"])
 
+    def first_arrival(s):
+        m = MA[0]
+        size_b(s, 0, 0, K)
+        offset(s, 0)
+        empty_b(s, 0)
+        empty_a(s, 0)
+        square(0, m, K)
+        square(0, 0, m)
+        make_g(s, 1)
+        over(m, K)
+        count_b(s, 0)
+        over(0, m)
+        count_a(s, 0)
+        make_sum(s, 0)
+
+    def next_arrival(s, k):
+        m = MA[k]
+        size_b(s, k, m, K)
+        empty_b(s, k)
+        size_b(s, k, 0, m)
+        empty_a(s, k)
+        if k == 1:
+            make_g(s, 2)
+        if k == 3:
+            far_list(s, 4)
+        make_sum(s, k)
+        if k == 2:
+            far_list(s, 3)
+        if k in (2, 3):
+            make_g(s, k + 1)
+
     def keys():
-        op("P", lambda: P.matmul(T.pv[:, 0:96], T.one[0:1, :], T.kc[0:1, :], True, False), ["one", "kc"], ["pv"])
-        for t in range(3):
-            sort_groups(lambda cp, t=t: T.pv[:, 3 * cp + t:96:6], t, t + 1, "pv", False)
+        for bank in KEYS:
+            op("P", lambda bank=bank: P.matmul(T[bank][:, 0:96], T.one[0:1, :], T.kc[0:1, :], True, False), ["one", "kc"], [bank])
+            for t in range(3):
+                sort_groups(lambda cp, t=t, bank=bank: T[bank][:, 3 * cp + t:96:6], t, t + 1, bank, False)
 
     def hold(s):
-        op("A", lambda: S.activation(win("held", T["e%d" % s][:]), T["sh%d" % s][:], Fn.Silu), ["sh%d" % s, "e%d" % s], ["held"])
+        op("A", lambda: S.activation(win("st", T["e%d" % s][:], 3 * W, 4 * W), T["sh%d" % s][:], Fn.Silu),
+           ["sh%d" % s, "e%d" % s], ["held"])
+        sem = "hd%d" % s
+        op("S", lambda: Y.dma_start(T.st[0::16, 2 * W:3 * W], T.st[0::16, 3 * W:4 * W]).then_inc(T.sem[sem], 16),
+           ["held"], ["st"], (sem, 16))
 
     def election(s):
-        ek, en = "e%d" % s, "e%d" % (s + 1)
-        old, oldk = (T.d0[:], "d0") if s == 0 else (T.dn0[:, 2::3], "dn0")
+        old, oldk = (T.d0[:], "d0") if s == 0 else (T.dn0[:, 3::4], "dn0")
         mark, half = T["sh%d" % s], MARK[s] / 2.0
-        cols = ((0, EL), (EL, K))
-        for hf, (a, b) in enumerate(cols):
-            for k in range(3):
-                lst, lk, _h, _hk = arrival(s, k, a, b)
-                op("A", lambda k=k, lst=lst, a=a, b=b: S.activation(T.mm[:, k, a:b], win("bb", lst), Fn.Abs),
-                   ["bb", lk], ["m%d%d" % (k, hf)])
 
-        def max01(hf):
-            a, b = cols[hf]
-            op("V", lambda: V.tensor_tensor(T.pm[:, a:b], T.mm[:, 0, a:b], T.mm[:, 1, a:b], A.max),
-               ["m0%d" % hf, "m1%d" % hf, "pm"], ["pm%d" % hf] + (["pm"] if hf == 0 else []))
+        def sizes(hf, k):
+            a, b = hf * H, (hf + 1) * H
+            lst, lk, _h, _hk = arrival(s, k, a, b)
+            op("A", lambda: S.activation(T.mm[:, k, a:b], win("bb", lst), Fn.Abs), ["bb", lk], ["m%d%d" % (k, hf)])
 
-        def max2(hf):
-            a, b = cols[hf]
-            op("V", lambda: V.tensor_tensor(T.pm[:, a:b], T.pm[:, a:b], T.mm[:, 2, a:b], A.max),
-               ["pm%d" % hf, "m2%d" % hf, "pm"], ["pm%d" % hf])
+        def larger(hf, k):
+            a, b = hf * H, (hf + 1) * H
+            top = TOPS[hf]
+            if (hf, k) == (0, 1):
+                op("V", lambda: V.tensor_tensor(T[top][:, a:b], T.mm[:, 0, a:b], T.mm[:, 1, a:b], A.max), ["m00", "m10"], [top])
+            else:
+                op("V", lambda: V.tensor_tensor(T[top][:, a:b], T[top][:, a:b], T.mm[:, k, a:b], A.max),
+                   [top, "m%d%d" % (k, hf)], [top])
 
         def vote(hf, k):
-            a, b = cols[hf]
-            op("V", lambda: V.tensor_tensor(T.vv[:, a:b, k], T.pm[:, a:b], T.mm[:, k, a:b], A.is_equal),
-               ["pm%d" % hf, "m%d%d" % (k, hf), "pm"], ["v%d%d" % (k, hf)])
+            a, b = hf * H, (hf + 1) * H
+            op("V", lambda: V.tensor_tensor(T.vv[:, a:b, k], T[TOPS[hf]][:, a:b], T.mm[:, k, a:b], A.is_equal),
+               [TOPS[hf], "m%d%d" % (k, hf)], ["v%d%d" % (k, hf)])
 
         def votes(hf):
-            a, b = cols[hf]
+            a, b = hf * H, (hf + 1) * H
 
             def fn():
                 last = None
                 for i in range(16):
-                    last = P.matmul(T.pv[:, 3 * a // 16:3 * b // 16], T.sel[:, 15 - i:143 - i], T.vv[:, a + i:b:16, :],
-                                    False, hf == 1 and i == 15)
+                    last = P.matmul(T[KEYS[hf]][:, 48 * hf:48 * hf + 48], T.sel[:, 15 - i:143 - i], T.vv[:, a + i:b:16, :],
+                                    False, i == 15)
                 return last
-            op("P", fn, ["sel", "v0%d" % hf, "v1%d" % hf, "v2%d" % hf], ["pv"])
-        c_scatter(s, 3)
-        max01(0)
-        op("V", lambda: V.tensor_copy(T.bs[:, 2::3], old), [oldk, "bs"], ["bs3"])
-        max2(0)
-        vote(0, 0)
-        vote(0, 1)
-        max01(1)
-        vote(0, 2)
-        votes(0)
-        max2(1)
-        for k in range(3):
-            vote(1, k)
-        votes(1)
-        c_scatter(s, 4)
-        op("V", lambda: V.tensor_tensor_scan(T.ks[:], T.pat[:], T.pv[:, 0:96], 0.0, A.mult, A.max), ["pv", "pat"], ["ks"])
-        op("P", lambda: P.matmul(T.pv[:, 96:192], T.one[0:1, :], T.pat[0:1, :], True, False), ["one", "pat"], ["pv"])
-        op("V", lambda: V.tensor_scalar(T.lw[:, 0:32], T.ks[:, 2::3], 4 * W - 1, None, A.bitwise_and), ["ks"], ["lwL"])
-        op("V", lambda: V.tensor_scalar(T.lw[:, 32:64], T.ks[:, 2::3], W - 1, None, A.bitwise_and), ["ks"], ["lwW"])
-        op("V", lambda: V.tensor_copy(T.lw16[:], T.lw[:]), ["lwL", "lwW"], ["lw16"])
-        op("A", lambda: S.activation(win("st", T.lw16[:, 0:32], 0, 3 * W), mark[:], Fn.Silu), ["lw16", "sh%d" % s], ["st"])
-        op("V", lambda: V.tensor_scalar(T.l1[:], T.lw[:, 0:32], 2 * W, None, A.min), ["lwL"], ["l1"])
-        op("V", lambda: V.tensor_scalar(T.l2[:], T.lw[:, 0:32], W, None, A.min), ["lwL"], ["l2"])
-        op("V", lambda: V.tensor_scalar(T.hg[:], win("held", T.lw16[:, 32:64]), half, half, A.is_le, A.mult),
-           ["held", "lw16"], ["hg"])
-        op("V", lambda: V.tensor_tensor(T.bs[:, 0::3], T.lw[:, 32:64], old, A.subtract), ["lwW", oldk, "bs"], ["bs0"])
-        c_scatter(s, 5)
-        op("A", lambda: S.activation(T.lk[:, :, 1], win("st", T.l1[:], W, 3 * W + 8), Fn.Relu, bias=-1.0, scale=1.0 / half),
-           ["st", "stz", "l1"], ["lkA"])
-        op("V", lambda: V.tensor_tensor(T.lk[:, :, 2], win("st", T.l2[:], 2 * W, 3 * W + 8), T.hg[:], A.is_ge),
-           ["st", "stz", "l2", "hg"], ["lkB"])
+            op("P", fn, ["sel", "v0%d" % hf, "v1%d" % hf, "v2%d" % hf], [KEYS[hf]])
+
+        def elect(hf):
+            a, b = 48 * hf, 48 * hf + 48
+            op("V", lambda: V.tensor_tensor_scan(T.ks[:, a:b], T.pat[:, a:b], T[KEYS[hf]][:, a:b], 0.0, A.mult, A.max),
+               [KEYS[hf], "pat"], ["ks%d" % hf])
+
+        def unpack(hf):
+            op("V", lambda: V.tensor_scalar(T.lw[:, 16 * hf:16 * hf + 16], T.ks[:, 48 * hf + 2:48 * hf + 48:3], SELW - 1, None,
+                                            A.bitwise_and), ["ks%d" % hf], ["lw%d" % hf])
+
+        def stamp(hf):
+            a, b = 16 * hf, 16 * hf + 16
+            op("V", lambda: V.tensor_copy(T.l1[:, a:b], T.lw[:, a:b]), ["lw%d" % hf], ["l1%d" % hf])
+            op("A", lambda: S.activation(win("st", T.l1[:, a:b], 0, 3 * W), mark[:, 16 * a:16 * b], Fn.Silu),
+               ["l1%d" % hf, "sh%d" % s], ["st", "st1"])
 
         def look():
             last = None
             for i in range(16):
-                last = P.matmul(T.pv[:, 96:192], T.seln[:, 15 - i:143 - i], T.lk[:, i::16, :], False, i == 15)
+                last = P.matmul(T.pv[:, 97:224:2], T.seln[:, 15 - i:143 - i], T.lk[:, i::16, :], False, i == 15)
             return last
-        op("P", look, ["seln", "lk0", "lkA", "lkB"], ["pv"])
+
+        for k in range(3):
+            sizes(0, k)
+        sizes(1, 0)
+        sizes(1, 1)
+        op("A", lambda: S.activation(T[TOPS[1]][:, H:K], T.mm[:, 0, H:K], Fn.Copy), ["m01"], [TOPS[1]])
+        sizes(1, 2)
+        c_scatter(s, 3)
+        larger(0, 1)
+        larger(0, 2)
+        vote(0, 0)
+        vote(0, 1)
+        larger(1, 1)
+        vote(0, 2)
+        votes(0)
+        larger(1, 2)
+        vote(1, 0)
+        vote(1, 1)
+        elect(0)
+        vote(1, 2)
+        votes(1)
+        unpack(0)
+        op("V", lambda: V.tensor_copy(T.bs[:, 3::4], old), [oldk, "bs"], ["bs3"])
+        stamp(0)
+        op("P", lambda: P.matmul(T.pv[:, 96:224], T.one[0:1, :], T.pat4[0:1, :], True, False), ["one", "pat4"], ["pv"])
+        c_scatter(s, 4)
+        elect(1)
+        unpack(1)
+        op("V", lambda: V.tensor_scalar(T.wish[:], T.ks[:, 2::3], W - 1, None, A.bitwise_and), ["ks0", "ks1"], ["wish"])
+        stamp(1)
+        op("V", lambda: V.tensor_scalar(T.l2[:], T.lw[:], 2 * W, None, A.min), ["lw0", "lw1"], ["l2"])
+        op("V", lambda: V.tensor_tensor(T.bs[:, 0::4], T.wish[:], old, A.subtract), ["wish", oldk, "bs"], ["bs0"])
+        c_scatter(s, 5)
+        op("A", lambda: S.activation(T.lk[:, :, 0], win("st", T.l1[:], W, 4 * W), Fn.Relu, bias=-1.0, scale=1.0 / half),
+           ["st", "held", "l10", "l11"], ["lkA"])
+        op("V", lambda: V.tensor_scalar(T.lk[:, :, 1], win("st", T.l2[:], 2 * W, 4 * W + 8), half, None, A.is_ge),
+           ["st", "held", "l2"], ["lkB"])
+        op("P", look, ["seln", "lkA", "lkB"], ["pv"])
         c_scatter(s, 6)
-        dn = "dn%d" % s
-        op("V", lambda: V.tensor_tensor_scan(T[dn][:], T.pv[:, 96:192], T.bs[:], 0.0, A.mult, A.add),
+        dn, en = "dn%d" % s, "e%d" % (s + 1)
+        op("V", lambda: V.tensor_tensor_scan(T[dn][:], T.pv[:, 96:224], T.bs[:], 0.0, A.mult, A.add),
            ["pv", "bs", "bs0", "bs3"], [dn])
-        op("V", lambda: V.tensor_copy(T[en][:], T[dn][:, 2::3]), [dn], [en])
+        op("V", lambda: V.tensor_copy(T[en][:], T[dn][:, 3::4]), [dn], [en])
 
     for s in range(RO):
         last = s == RO - 1
         if s == 0:
-            zero_b(s)
-            take_b(s, 0, K)
-            delta(s, 0, K)
-            table_gather(s)
             limit(0)
-            table_turn()
+            take_b(s)
             limit(1)
-            make_h(s, 0, K)
-            limit(2)
-        else:
-            take_b(s, 0, K)
             zero_b(s)
-            table_gather(s)
-            delta(s, 0, K)
-            table_turn()
-            make_h(s, 0, K)
-        list0()
-        send(s)
-        if s == 0:
+            delta(s)
+            limit(2)
+            table_lists(s)
+            make_h(s)
+            hop_lists()
+            send(s)
             limit(3)
-            limit(4)
-        make_g(s, 0)
+        else:
+            take_b(s)
+            zero_b(s)
+            table_lists(s)
+            delta(s)
+            hop_lists()
+            make_h(s)
+            send(s)
+        make_g(s, 0, MA[0], K)
+        make_g(s, 0, 0, MA[0])
         if s == 0:
-            gfill(T.cc[:, 64:W], [[0, W - 64]], 0, ["cR"])
-            gfill(T.kc[:], [[0, 32], [-W, 3]], 2 * W, ["kc"])
-            gfill(T.one[:], [[0, 128]], 1, ["one"])
-            gfill(T.sel[:], [[0, 144]], int(SELW), ["sel"])
-            gfill(T.seln[:], [[0, 144]], -1, ["seln"])
-            gfill(T.pat[:], [[0, 96]], 1, ["pat"])
-            gkeep("sel", [[0, 9], [1, 16]], A.is_equal, -15, 0)
-            gkeep("seln", [[0, 9], [1, 16]], A.is_equal, -15, 0)
-            gkeep("pat", [[0, 32], [1, 3]], A.not_equal, 0, 0)
-            gkeep("sel", [[1, 144]], A.is_ge, 0, -1)
-            gkeep("seln", [[1, 144]], A.is_equal, -15, -1)
-            gkeep("sel", [[-1, 144]], A.is_ge, 15, 1)
-            gfill(T.bs[:], [[0, 96]], 0, ["bs"])
-            gfill(T.lk[:, :, 0], [[0, K]], 0, ["lk0"])
-            gfill(T.held[:], [[0, W]], 0, ["held"])
-            gfill(T.sh0[:], [[0, K]], MARK[0], ["sh0"])
-            gfill(T.st[:, W:3 * W + 8], [[0, 2 * W + 8]], 0, ["st", "stz"])
-            gfill(T.sh1[:], [[0, K]], MARK[1], ["sh1"])
-        empty(s, 0, True)
-        size(0)
-        list12()
-        make_g(s, 1)
-        over()
-        count_a(s, 0, False)
-        make_sum(s, 0)
+            later_constants()
+        first_arrival(s)
         for k in range(5):
             if k > 0:
-                empty(s, k)
-                if k < 4:
-                    make_g(s, k + 1)
-                make_sum(s, k)
-            if k < 4:
-                size(k + 1, SQ if k else 0, K)
-            else:
+                next_arrival(s, k)
+            if k == 4:
                 c_scatter(s, 2)
                 if last:
                     op("S", lambda: Y.dma_start(T.yc[:], T.cc[:]).then_inc(T.sem.o_c, 16), C2, ["yc"], ("o_c", 16))
             mask_b(s, k)
             put(s, k)
             if k < 4:
-                m = MA[k + 1]
-                if k and SQ:
-                    size(k + 1, 0, SQ)
-                if MODE:
-                    over(m, K)
-                    count_b(s, k + 1)
-                    over(0, m)
-                else:
-                    over()
-                    count_b(s, k + 1)
+                square(k + 1)
+                over()
+                offset(s, k + 1)
+                count_b(s, k + 1)
                 count_a(s, k + 1)
-                if s > 0 and k in CG:
-                    c_gather(s, *CG[k])
-                enough(s, k + 1)
-            if k == 3 and not last:
-                keys()
-            if k == 4 and not last:
-                hold(s)
+                if s > 0 and k < 2:
+                    c_gather(s, k * H, (k + 1) * H)
         if not last:
+            keys()
+            hold(s)
             election(s)
 
     op("S", lambda: Y.dma_start(T.yb[:], T.bb[:]).then_inc(T.sem.o_b, 16), ["bb"], ["yb"], ("o_b", 16))

from concourse.mybir import AluOpType, ActivationFunctionType

W, K, RO = 2048, 512, 3
F32, BF, F16, I32, U16 = "float32", "bfloat16", "float16", "int32", "uint16"
MSG = K + 64
H = K // 2
MA = [256, 128, 128, 128, 192]
CUTS = [[0, 0, 0, 64, 192, 256, 384, 512], [0, 0, 0, 64, 192, 256, 384, 512], [0, 128, 256, 512]]
TBV = 1360
ROWS = 3
UNIT = 2.0 ** -20
BIG = 384
TOP = 2.0 - 2.0 ** -13
SELW = 8192
MARK = (32, 512)

SCRATCH = {
    "bb": ("sbuf", [128, W], F32), "cc": ("sbuf", [128, W], F32),
    "tb": ("sbuf", [128, W], I32), "st": ("sbuf", [128, 4 * W + 8], F32),
    "b0s": ("sbuf", [128, W], BF), "ws": ("sbuf", [128, W], BF), "recs": ("sbuf", [128, W], BF),
    "row": ("sbuf", [128, 128], F32), "ths": ("sbuf", [128, 8], F32), "aux": ("sbuf", [128, 8], F32),
    "rough": ("sbuf", [128, 16], BF), "sc": ("sbuf", [128, 8], F32), "lim": ("sbuf", [128, 8], F32),
    "zin": ("sbuf", [128, K], F32), "sh0": ("sbuf", [128, K], F32), "sh1": ("sbuf", [128, K], F32),
    "ones": ("sbuf", [128, 160], F32), "jj": ("sbuf", [128, 160], F32),
    "pe": ("sbuf", [128, 160], F16), "po": ("sbuf", [128, 160], F16),
    "bd0": ("sbuf", [128, 2, 128], BF), "bd1": ("sbuf", [128, 2, 128], BF), "bd": ("sbuf", [128, 2, 128], BF),
    "sel": ("sbuf", [128, 144], BF), "seln": ("sbuf", [128, 144], BF),
    "one": ("sbuf", [128, 128], BF), "cst": ("sbuf", [128, 2, K], BF), "kc": ("sbuf", [128, 96], BF),
    "pat": ("sbuf", [128, 96], BF), "pat4": ("sbuf", [128, 128], BF),
    "d0": ("sbuf", [128, 32], I32), "e0": ("sbuf", [128, 32], U16), "e1": ("sbuf", [128, 32], U16),
    "e2": ("sbuf", [128, 32], U16),
    "xl": ("sbuf", [128, 96], U16), "xu": ("sbuf", [128, 32], U16), "xd": ("sbuf", [128, 32], U16),
    "l1": ("sbuf", [128, 32], U16), "l2": ("sbuf", [128, 32], U16),
    "nb": ("sbuf", [128, K], F32), "dl": ("sbuf", [128, K], F32), "cd": ("sbuf", [128, K], F32),
    "tg": ("sbuf", [128, K], F16), "tr": ("sbuf", [128, 16, 2, 16], F16),
    "g0": ("sbuf", [128, K], F32), "g1": ("sbuf", [128, K], F32), "g2": ("sbuf", [128, K], F32),
    "sm": ("sbuf", [128, K], F32), "mk": ("sbuf", [128, K], F32),
    "sq": ("sbuf", [128, K], F32), "ov": ("sbuf", [128, K], BF), "ab": ("sbuf", [128, K], BF),
    "mm": ("sbuf", [128, 3, K], F32), "vv": ("sbuf", [128, K, 3], BF),
    "ks": ("sbuf", [128, 96], I32), "lw": ("sbuf", [128, 32], I32), "wish": ("sbuf", [128, 32], I32),
    "bs": ("sbuf", [128, 128], F32), "dn0": ("sbuf", [128, 128], F32), "dn1": ("sbuf", [128, 128], F32),
    "lk": ("sbuf", [128, K, 2], BF),
    "pa0": ("psum", [128, K], F32), "pb0": ("psum", [128, K], F32),
    "pa1": ("psum", [128, K], F32), "pb1": ("psum", [128, K], F32),
    "pc": ("psum", [128, K], F32), "pm": ("psum", [128, K], F32),
    "pl": ("psum", [128, 256, 2], F32), "pv": ("psum", [128, K], F32),
}
for _s in range(RO):
    for _n in ("snd", "lu", "lr", "ld"):
        SCRATCH["%s%d" % (_n, _s)] = ("sbuf", [128, MSG], F32)
PSUM = ("pa0", "pb0", "pa1", "pb1", "pc", "pl", "pm", "pv")
KEYS = ("pv", "pc")
TOPS = ("pm", "pb0")

SEMAPHORES = ["cV", "cA", "cP", "cG", "l_wk", "l_th", "l_b0", "l_rec", "l_w", "l_tb", "sent", "o_c", "o_b", "hd0", "hd1"]
for _s in range(RO):
    SEMAPHORES += ["au%d" % _s, "ad%d" % _s, "rot%d" % _s]


def new_plan():
    return {"ops": [], "writer": {}, "readers": {}, "known": {q: ({}, set()) for q in "VAPGS"}, "n": {q: 0 for q in "VAPG"}}


def add(plan, q, fn, reads=(), writes=(), dma=None):
    op = {"q": q, "fn": fn, "dma": dma, "waits": [], "need": False, "id": len(plan["ops"])}
    if dma is None:
        op["idx"] = plan["n"][q]
        plan["n"][q] += 1
    deps = []
    for k in reads:
        if k in plan["writer"]:
            deps.append(plan["writer"][k])
        if k in PSUM:
            deps += [r for r in plan["readers"].get(k, []) if r["q"] != q]
    for k in writes:
        if k in plan["writer"]:
            deps.append(plan["writer"][k])
        deps += plan["readers"].get(k, [])
    if q is not None:
        cnt, done = plan["known"][q]
        deps.sort(key=lambda d: -d["id"])
        for d in deps:
            if d["dma"] is None:
                if d["q"] == "P" and q == "P":
                    continue
                if cnt.get(d["q"], -1) >= d["idx"]:
                    continue
                cnt[d["q"]] = d["idx"]
            else:
                if d["id"] in done:
                    continue
                done.add(d["id"])
            d["need"] = True
            op["waits"].append(d)
            for e, v in d["clock"][0].items():
                if cnt.get(e, -1) < v:
                    cnt[e] = v
            done.update(d["clock"][1])
        op["clock"] = (dict(cnt), set(done))
    else:
        op["clock"] = ({}, set())
    for k in reads:
        plan["readers"].setdefault(k, []).append(op)
    for k in writes:
        plan["writer"][k] = op
        plan["readers"][k] = []
    plan["ops"].append(op)
    return op


def emit(plan, g, T):
    qs = {"V": g.vector, "A": g.scalar, "P": g.tensor, "G": g, "S": g.sync}
    cnt = {q: 0 for q in "VAPG"}
    for op in plan["ops"]:
        if op["dma"] is None and op["need"]:
            cnt[op["q"]] += 1
            op["val"] = cnt[op["q"]]
    for op in plan["ops"]:
        if op["q"] is None:
            continue
        for d in op["waits"]:
            if d["dma"] is None:
                qs[op["q"]].wait_ge(T.sem["c" + d["q"]], d["val"])
            else:
                qs[op["q"]].wait_ge(T.sem[d["dma"][0]], d["dma"][1])
        ins = op["fn"]()
        if op["dma"] is None and op["need"]:
            ins.then_inc(T.sem["c" + op["q"]], 1)


def rank_program(g, core, T, topo):
    rank = T.rank_of(core)
    if rank is None:
        return
    n = len(T.cores)
    A, Fn = AluOpType, ActivationFunctionType
    V, S, P, Y = g.vector, g.scalar, g.tensor, g.sync
    plan = new_plan()
    C2, TB = ["cL", "cR"], ["tbL", "tbR"]
    bda, bdb = T.bd[:, 0, :], T.bd[:, 1, :]

    def op(q, fn, reads=(), writes=(), dma=None):
        return add(plan, q, fn, reads, writes, dma)

    def win(name, lst, a=0, b=W):
        return T[name][:, a:b].indirect(lst)

    def part(name, a=0, b=K):
        return ["%s_%d" % (name, i) for i in range(a // 64, (b + 63) // 64)]

    def load(q, eng, dst, src, sem, key):
        op(q, lambda: eng.dma_start(dst, src).then_inc(T.sem[sem], 16), [], [key], (sem, 16))

    def gfill(ap, pattern, val, keys):
        op("G", lambda: g.iota(ap, pattern, val, 0, allow_small_or_imprecise_dtypes=True), [], keys)

    def gkeep(dst, src, pattern, test, base, mult, keys=None):
        op("G", lambda: g.affine_select(T[dst][:], T[src][:], pattern, test, 0.0, base, mult), keys or [src], [dst])

    load("A", S, T.b0s[:], T.b0[:], "l_b0", "b0s")
    load("S", Y, T.d0[:], T.wk[:], "l_wk", "d0")
    load("S", Y, T.row[0:1, :], T.th[:], "l_th", "row")
    load("S", Y, T.recs[:], T.rec[:], "l_rec", "recs")
    op("V", lambda: V.memset(T.zin[:, 0:64], -128.0), [], ["zin0"])
    op("V", lambda: V.memset(T.tb[:, 0:TBV], 0), [], ["tbL"])
    op("V", lambda: V.memset(T.ones[:], 1.0), [], ["ones"])
    op("G", lambda: g.iota(T.tb[:, TBV:W], [[0, W - TBV]], 0, 0), [], ["tbR"])
    op("V", lambda: V.memset(T.bd0[:, 0, :], 2.0 ** 46), [], ["bd0a"])
    op("V", lambda: V.memset(T.bd0[:, 1, :], UNIT), [], ["bd0b"])
    op("P", lambda: P.transpose(T.pa0[:, 0:1], T.row[0:1, :], T.ones[0:1, 0:1]), ["row", "ones"], ["pa0"])

    def tables():
        for t in range(5):
            src = T.hop[:, t * W:(t + 1) * W] if t < 3 else (T.up[:] if t == 3 else T.dn[:])
            Y.dma_start(T.tb[ROWS * t::16, :], src).then_inc(T.sem.l_tb, 16)
    op("S", tables, [], TB, ("l_tb", 80))
    load("S", Y, T.ws[:], T.w[:], "l_w", "ws")

    gkeep("jj", "ones", [[1, 160]], A.is_equal, -16, -1)
    gkeep("bd1", "bd0", [[0, 2], [-16, 8], [0, 16]], A.is_ge, 0, 1, ["bd0a", "bd0b"])
    gkeep("pe", "jj", [[0, 5], [1, 2], [0, 16]], A.is_gt, 0, 0)
    gkeep("po", "jj", [[0, 5], [1, 2], [0, 16]], A.is_equal, 0, 0)
    gkeep("bd", "bd1", [[0, 2], [16, 8], [0, 16]], A.is_ge, 15, -1)
    gfill(T.one[0:1, :], [[0, 128]], 1, ["one"])
    for i, v in enumerate((15, BIG)):
        gfill(T.cst[0:1, i, min(MA):K], [[0, K - min(MA)]], v, ["cst%d" % i])
    op("A", lambda: S.activation(T.cc[:, 0:64], T.zin[:, 0:64], Fn.Silu), ["zin0"], ["cL"])
    ZIN = range(64, K, 160)
    for a in ZIN:
        op("A", lambda a=a: S.activation(T.zin[:, a:min(a + 160, K)], T.ones[:, 0:min(160, K - a)], Fn.Copy, scale=-128.0),
           ["ones"], ["zin%d" % a])
    op("A", lambda: S.activation(T.bb[:], T.b0s[:], Fn.Copy), ["b0s"], ["bb"])
    op("V", lambda: V.tensor_copy(T.e0[:], T.d0[:]), ["d0"], ["e0"])

    def limit(i):
        th, c = T.ths[:, 0:1], lambda j: T.aux[:, j:j + 1]
        if i == 0:
            op("V", lambda: V.reciprocal(c(0), T.pa0[:, 0:1]), ["pa0"], ["aux0"])
            op("V", lambda: V.tensor_copy(th, T.pa0[:, 0:1]), ["pa0"], ["ths"])
            op("V", lambda: V.tensor_scalar(T.rough[:, 0:1], c(0), TOP, None, A.mult), ["aux0"], ["rough"])
            op("V", lambda: V.tensor_scalar(c(1), c(0), TOP, None, A.mult), ["aux0"], ["aux1"])
        if i == 1:
            op("V", lambda: V.tensor_scalar(c(2), th, T.rough[:, 0:1], 2.0, A.mult, A.is_lt), ["ths", "rough"], ["aux2"])
        if i == 2:
            op("V", lambda: V.tensor_scalar(T.sc[:, 0:1], T.rough[:, 0:1], c(2), c(1), A.mult, A.max),
               ["aux1", "aux2", "rough"], ["sc"])
        if i == 3:
            op("A", lambda: S.activation(c(3), th, Fn.Square, scale=T.sc[:, 0:1]), ["ths", "sc"], ["aux3"])
            op("A", lambda: S.activation(T.lim[:, 0:1], c(3), Fn.Identity, bias=-2.0 ** -22, scale=-1.0), ["aux3"], ["lim"])

    def later_constants():
        gfill(T.cc[:, 64:W], [[0, W - 64]], 0, ["cR"])
        gfill(T.kc[:], [[0, 32], [-W, 3]], 2 * W, ["kc"])
        gfill(T.st[:, 2 * W:4 * W + 8], [[0, 2 * W + 8]], 0, ["held", "st"])
        gfill(T.sh0[:], [[0, K]], MARK[0], ["sh0"])
        gfill(T.sel[:], [[0, 144]], SELW, ["sel"])
        gfill(T.seln[:], [[0, 144]], -1, ["seln"])
        gfill(T.pat[:], [[0, 96]], 1, ["pat"])
        gkeep("sel", "sel", [[0, 9], [1, 16]], A.is_equal, -15, 0)
        gkeep("seln", "seln", [[0, 9], [1, 16]], A.is_equal, -15, 0)
        gkeep("pat", "pat", [[0, 32], [1, 3]], A.not_equal, 0, 0)
        gkeep("sel", "sel", [[1, 144]], A.is_ge, 0, -1)
        gkeep("seln", "seln", [[1, 144]], A.is_equal, -15, -1)
        gkeep("sel", "sel", [[-1, 144]], A.is_ge, 15, 1)
        gfill(T.bs[:], [[0, 128]], 0, ["bs"])
        gfill(T.pat4[:], [[0, 128]], 1, ["pat4"])
        gkeep("pat4", "pat4", [[0, 32], [1, 4]], A.not_equal, 0, 0)
        gfill(T.st[:, W:2 * W], [[0, W]], 0, ["st1"])
        gfill(T.sh1[:], [[0, K]], MARK[1], ["sh1"])

    def take_b(s):
        ek = "e%d" % s
        if s == 0:
            op("V", lambda: V.tensor_scalar(T.nb[:], win("b0s", T[ek][:]), -1.0, None, A.mult), ["b0s", ek], ["nb"])
        else:
            op("A", lambda: S.activation(T.nb[:], win("bb", T[ek][:]), Fn.Copy, scale=-1.0), ["bb", ek], ["nb"])

    def zero_b(s):
        op("A", lambda: S.activation(win("bb", T["e%d" % s][:]), T.zin[:], Fn.Silu),
           ["zin0", "e%d" % s] + ["zin%d" % a for a in ZIN], ["bb"])

    def delta(s):
        op("V", lambda: V.tensor_tensor(T.dl[:], win("recs", T["e%d" % s][:]), T.nb[:], A.mult), ["recs", "e%d" % s, "nb"], ["dl"])

    def make_h(s):
        op("V", lambda: V.tensor_tensor(T["snd%d" % s][:, 0:K], win("ws", T["e%d" % s][:]), T.dl[:], A.mult),
           ["ws", "e%d" % s, "dl"], ["h%d" % s])

    def sort_groups(out, t0, t1, key, opens=True):
        def fn():
            last = None
            for cp in range(2):
                m = T.pe if cp == 0 else T.po
                for gp in range(2):
                    a = 16 - 16 * (gp - cp)
                    rhs = T.tr[:, :, gp, ROWS * t0:ROWS * (t1 - 1) + 1:ROWS]
                    last = P.matmul(out(cp), m[:, a:a + 128], rhs, opens and gp == 0, opens and gp == 1)
            return last
        op("P", fn, ["tr", "pe", "po"], [key])

    def table_lists(s):
        op("V", lambda: V.tensor_copy(T.tg[:], win("tb", T["e%d" % s][:])), TB + ["e%d" % s], ["tg"])
        op("V", lambda: V.transpose(T.tr[:], T.tg[:]), ["tg"], ["tr"])
        for t in range(3):
            sort_groups(lambda cp, t=t: T.pm[:, 32 * t + cp:32 * t + 32:2], t, t + 1, "pm")
        sort_groups(lambda cp: T.pl[:, cp:32:2, :], 3, 5, "pl")

    def hop_lists():
        op("V", lambda: V.tensor_copy(T.xl[:], T.pm[:, 0:96]), ["pm"], ["xl"])

    def send(s):
        snd = T["snd%d" % s]
        op("V", lambda: V.tensor_copy(snd[:, K:MSG], T.pl[:, 0:32, :]), ["pl"], ["sl%d" % s])
        for dst, land, sem in ((T.cores[(rank + 1) % n], "lu", "au"), (T.cores[(rank - 1) % n], "ld", "ad")):
            def write(dst=dst, land=land, sem=sem):
                rid, pid, _e = topo.addr(dst)
                g.remote_dma(T["%s%d" % (land, s)][:], snd[:], T.sem["%s%d" % (sem, s)], T.sem.sent, pid, rid,
                             topo.mask(core, dst))
            op("G", write, ["h%d" % s, "sl%d" % s], [], ("sent", 0))
        op(None, None, [], ["lu%d" % s], ("au%d" % s, len(topo.engines(T.cores[(rank - 1) % n], core))))
        op(None, None, [], ["ld%d" % s], ("ad%d" % s, len(topo.engines(T.cores[(rank + 1) % n], core))))

        def turn():
            Y.dma_start(T["lr%d" % s][16:128, :], T["lu%d" % s][0:112, :]).then_inc(T.sem["rot%d" % s], 16)
            Y.dma_start(T["lr%d" % s][0:16, :], T["lu%d" % s][112:128, :]).then_inc(T.sem["rot%d" % s], 16)
        op("S", turn, ["lu%d" % s], ["lr%d" % s], ("rot%d" % s, 32))

    def c_scatter(s, i):
        if i + 1 >= len(CUTS[s]) or CUTS[s][i] == CUTS[s][i + 1]:
            return
        a, b = CUTS[s][i], CUTS[s][i + 1]
        lst, ek = T["e%d" % s][:, a // 16:b // 16], "e%d" % s
        if s == 0:
            op("V", lambda: V.tensor_copy(win("cc", lst), T.dl[:, a:b]), ["dl", ek], C2)
        else:
            op("V", lambda: V.tensor_tensor(win("cc", lst), T.cd[:, a:b], T.dl[:, a:b], A.add),
               ["dl", ek] + part("cd", a, b), C2)

    def c_gather(s, a, b):
        op("A", lambda: S.activation(T.cd[:, a:b], win("cc", T["e%d" % s][:, a // 16:b // 16]), Fn.Copy),
           C2 + ["e%d" % s], part("cd", a, b))

    def arrival(s, k, a=0, b=K):
        a16, b16 = a // 16, b // 16
        if k < 3:
            return T.xl[:, 32 * k + a16:32 * k + b16], "xl", T["snd%d" % s][:, a:b], "h%d" % s
        if k == 3:
            return T.xu[:, a16:b16], "xu", T["lr%d" % s][:, a:b], "lr%d" % s
        return T.xd[:, a16:b16], "xd", T["ld%d" % s][:, a:b], "ld%d" % s

    def far_list(s, k):
        _l, lk, _h, hk = arrival(s, k)
        op("V", lambda: V.tensor_copy(T[lk][:], T[hk][:, K + k - 3:MSG:2]), [hk], [lk])

    def make_g(s, k, a=0, b=K):
        lst, lk, h, hk = arrival(s, k, a, b)
        gb = "g%d" % (k % 3)
        op("V", lambda: V.tensor_tensor(T[gb][:, a:b], win("ws", lst), h, A.mult), ["ws", lk, hk], part(gb, a, b))

    def banks(s, k):
        par = (5 * s + k) % 2
        return "pa%d" % par, "pb%d" % par

    def square(k, a=0, b=K):
        gb = "g%d" % (k % 3)
        op("A", lambda: S.activation(T.sq[:, a:b], T[gb][:, a:b], Fn.Square, scale=T.sc[:, 0:1]),
           part(gb, a, b) + ["sc"], part("sq", a, b))

    def over(a=0, b=K):
        op("A", lambda: S.activation(T.ov[:, a:b], T.sq[:, a:b], Fn.Sign, bias=T.lim[:, 0:1]),
           part("sq", a, b) + ["lim"], part("ov", a, b))

    def size_b(s, k, a, b):
        lst, lk, _h, _hk = arrival(s, k, a, b)
        op("A", lambda: S.activation(T.ab[:, a:b], win("bb", lst), Fn.Abs, scale=2.0 ** 64), ["bb", lk], part("ab", a, b))

    def offset(s, k):
        pb, m = banks(s, k)[1], MA[k]
        op("P", lambda: P.matmul(T[pb][:, 0:K - m], T.bd0[0:1, 1, :], T.cst[0:1, 0, m:K], True, False), ["bd0b", "cst0"], [pb])

    def count_b(s, k):
        pb, m = banks(s, k)[1], MA[k]

        def fn():
            P.matmul(T[pb][:, 0:K - m], bdb, T.ov[:, m:K], False, False)
            return P.matmul(T[pb][:, 0:K - m], T.one[0:1, :], T.cst[0:1, 1, m:K], False, k == 0)
        op("P", fn, part("ov", m, K) + ["bd", "one", "cst1"], [pb])

    def count_a(s, k):
        pa, m = banks(s, k)[0], MA[k]
        op("P", lambda: P.matmul(T[pa][:, 0:m], bdb, T.ov[:, 0:m], k > 0, k == 0), part("ov", 0, m) + ["bd"], [pa])

    def empty_b(s, k):
        pb, m = banks(s, k)[1], MA[k]
        op("P", lambda: P.matmul(T[pb][:, 0:K - m], bda, T.ab[:, m:K], False, k > 0), part("ab", m, K) + ["bd"], [pb])

    def empty_a(s, k):
        pa, m = banks(s, k)[0], MA[k]
        op("P", lambda: P.matmul(T[pa][:, 0:m], bda, T.ab[:, 0:m], k == 0, k > 0), part("ab", 0, m) + ["bd"], [pa])

    def make_sum(s, k):
        lst, lk, _h, _hk = arrival(s, k)
        gb = "g%d" % (k % 3)
        op("V", lambda: V.tensor_tensor(T.sm[:], win("bb", lst), T[gb][:], A.add), ["bb", lk] + part(gb), ["sm"])

    def mask_b(s, k):
        pb, m = banks(s, k)[1], MA[k]
        op("A", lambda: S.activation(T.mk[:, m:K], T[pb][:, 0:K - m], Fn.Sign, bias=-float(BIG)), [pb], ["mkB"])

    def put(s, k):
        lst, lk, _h, _hk = arrival(s, k)
        pa, m = banks(s, k)[0], MA[k]
        op("V", lambda: V.tensor_scalar(T.mk[:, 0:m], T[pa][:, 0:m], UNIT, None, A.is_gt), [pa], ["mkA"])
        if k in (1, 3):
            c_scatter(s, k // 2)
        op("V", lambda: V.tensor_tensor(win("bb", lst), T.sm[:], T.mk[:], A.mult), ["sm", "mkA", "mkB", lk], ["bb"])

    def first_arrival(s):
        m = MA[0]
        size_b(s, 0, 0, K)
        offset(s, 0)
        empty_b(s, 0)
        empty_a(s, 0)
        square(0, m, K)
        square(0, 0, m)
        make_g(s, 1)
        over(m, K)
        count_b(s, 0)
        over(0, m)
        count_a(s, 0)
        make_sum(s, 0)

    def next_arrival(s, k):
        m = MA[k]
        size_b(s, k, m, K)
        empty_b(s, k)
        size_b(s, k, 0, m)
        empty_a(s, k)
        if k == 1:
            make_g(s, 2)
        if k == 3:
            far_list(s, 4)
        make_sum(s, k)
        if k == 2:
            far_list(s, 3)
        if k in (2, 3):
            make_g(s, k + 1)

    def keys():
        for bank in KEYS:
            op("P", lambda bank=bank: P.matmul(T[bank][:, 0:96], T.one[0:1, :], T.kc[0:1, :], True, False), ["one", "kc"], [bank])
            for t in range(3):
                sort_groups(lambda cp, t=t, bank=bank: T[bank][:, 3 * cp + t:96:6], t, t + 1, bank, False)

    def hold(s):
        op("A", lambda: S.activation(win("st", T["e%d" % s][:], 3 * W, 4 * W), T["sh%d" % s][:], Fn.Silu),
           ["sh%d" % s, "e%d" % s], ["held"])
        sem = "hd%d" % s
        op("S", lambda: Y.dma_start(T.st[0::16, 2 * W:3 * W], T.st[0::16, 3 * W:4 * W]).then_inc(T.sem[sem], 16),
           ["held"], ["st"], (sem, 16))

    def election(s):
        old, oldk = (T.d0[:], "d0") if s == 0 else (T.dn0[:, 3::4], "dn0")
        mark, half = T["sh%d" % s], MARK[s] / 2.0

        def sizes(hf, k):
            a, b = hf * H, (hf + 1) * H
            lst, lk, _h, _hk = arrival(s, k, a, b)
            op("A", lambda: S.activation(T.mm[:, k, a:b], win("bb", lst), Fn.Abs), ["bb", lk], ["m%d%d" % (k, hf)])

        def larger(hf, k):
            a, b = hf * H, (hf + 1) * H
            top = TOPS[hf]
            if (hf, k) == (0, 1):
                op("V", lambda: V.tensor_tensor(T[top][:, a:b], T.mm[:, 0, a:b], T.mm[:, 1, a:b], A.max), ["m00", "m10"], [top])
            else:
                op("V", lambda: V.tensor_tensor(T[top][:, a:b], T[top][:, a:b], T.mm[:, k, a:b], A.max),
                   [top, "m%d%d" % (k, hf)], [top])

        def vote(hf, k):
            a, b = hf * H, (hf + 1) * H
            op("V", lambda: V.tensor_tensor(T.vv[:, a:b, k], T[TOPS[hf]][:, a:b], T.mm[:, k, a:b], A.is_equal),
               [TOPS[hf], "m%d%d" % (k, hf)], ["v%d%d" % (k, hf)])

        def votes(hf):
            a, b = hf * H, (hf + 1) * H

            def fn():
                last = None
                for i in range(16):
                    last = P.matmul(T[KEYS[hf]][:, 48 * hf:48 * hf + 48], T.sel[:, 15 - i:143 - i], T.vv[:, a + i:b:16, :],
                                    False, i == 15)
                return last
            op("P", fn, ["sel", "v0%d" % hf, "v1%d" % hf, "v2%d" % hf], [KEYS[hf]])

        def elect(hf):
            a, b = 48 * hf, 48 * hf + 48
            op("V", lambda: V.tensor_tensor_scan(T.ks[:, a:b], T.pat[:, a:b], T[KEYS[hf]][:, a:b], 0.0, A.mult, A.max),
               [KEYS[hf], "pat"], ["ks%d" % hf])

        def unpack(hf):
            op("V", lambda: V.tensor_scalar(T.lw[:, 16 * hf:16 * hf + 16], T.ks[:, 48 * hf + 2:48 * hf + 48:3], SELW - 1, None,
                                            A.bitwise_and), ["ks%d" % hf], ["lw%d" % hf])

        def stamp(hf):
            a, b = 16 * hf, 16 * hf + 16
            op("V", lambda: V.tensor_copy(T.l1[:, a:b], T.lw[:, a:b]), ["lw%d" % hf], ["l1%d" % hf])
            op("A", lambda: S.activation(win("st", T.l1[:, a:b], 0, 3 * W), mark[:, 16 * a:16 * b], Fn.Silu),
               ["l1%d" % hf, "sh%d" % s], ["st", "st1"])

        def look():
            last = None
            for i in range(16):
                last = P.matmul(T.pv[:, 97:224:2], T.seln[:, 15 - i:143 - i], T.lk[:, i::16, :], False, i == 15)
            return last

        for k in range(3):
            sizes(0, k)
        sizes(1, 0)
        sizes(1, 1)
        op("A", lambda: S.activation(T[TOPS[1]][:, H:K], T.mm[:, 0, H:K], Fn.Copy), ["m01"], [TOPS[1]])
        sizes(1, 2)
        c_scatter(s, 3)
        larger(0, 1)
        larger(0, 2)
        vote(0, 0)
        vote(0, 1)
        larger(1, 1)
        vote(0, 2)
        votes(0)
        larger(1, 2)
        vote(1, 0)
        vote(1, 1)
        elect(0)
        vote(1, 2)
        votes(1)
        unpack(0)
        op("V", lambda: V.tensor_copy(T.bs[:, 3::4], old), [oldk, "bs"], ["bs3"])
        stamp(0)
        op("P", lambda: P.matmul(T.pv[:, 96:224], T.one[0:1, :], T.pat4[0:1, :], True, False), ["one", "pat4"], ["pv"])
        c_scatter(s, 4)
        elect(1)
        unpack(1)
        op("V", lambda: V.tensor_scalar(T.wish[:], T.ks[:, 2::3], W - 1, None, A.bitwise_and), ["ks0", "ks1"], ["wish"])
        stamp(1)
        op("V", lambda: V.tensor_scalar(T.l2[:], T.lw[:], 2 * W, None, A.min), ["lw0", "lw1"], ["l2"])
        op("V", lambda: V.tensor_tensor(T.bs[:, 0::4], T.wish[:], old, A.subtract), ["wish", oldk, "bs"], ["bs0"])
        c_scatter(s, 5)
        op("A", lambda: S.activation(T.lk[:, :, 0], win("st", T.l1[:], W, 4 * W), Fn.Relu, bias=-1.0, scale=1.0 / half),
           ["st", "held", "l10", "l11"], ["lkA"])
        op("V", lambda: V.tensor_scalar(T.lk[:, :, 1], win("st", T.l2[:], 2 * W, 4 * W + 8), half, None, A.is_ge),
           ["st", "held", "l2"], ["lkB"])
        op("P", look, ["seln", "lkA", "lkB"], ["pv"])
        c_scatter(s, 6)
        dn, en = "dn%d" % s, "e%d" % (s + 1)
        op("V", lambda: V.tensor_tensor_scan(T[dn][:], T.pv[:, 96:224], T.bs[:], 0.0, A.mult, A.add),
           ["pv", "bs", "bs0", "bs3"], [dn])
        op("V", lambda: V.tensor_copy(T[en][:], T[dn][:, 3::4]), [dn], [en])

    for s in range(RO):
        last = s == RO - 1
        if s == 0:
            limit(0)
            take_b(s)
            limit(1)
            zero_b(s)
            delta(s)
            limit(2)
            table_lists(s)
            make_h(s)
            hop_lists()
            send(s)
            limit(3)
        else:
            take_b(s)
            zero_b(s)
            table_lists(s)
            delta(s)
            hop_lists()
            make_h(s)
            send(s)
        make_g(s, 0, MA[0], K)
        make_g(s, 0, 0, MA[0])
        if s == 0:
            later_constants()
        first_arrival(s)
        for k in range(5):
            if k > 0:
                next_arrival(s, k)
            if k == 4:
                c_scatter(s, 2)
                if last:
                    op("S", lambda: Y.dma_start(T.yc[:], T.cc[:]).then_inc(T.sem.o_c, 16), C2, ["yc"], ("o_c", 16))
            mask_b(s, k)
            put(s, k)
            if k < 4:
                square(k + 1)
                over()
                offset(s, k + 1)
                count_b(s, k + 1)
                count_a(s, k + 1)
                if s > 0 and k < 2:
                    c_gather(s, k * H, (k + 1) * H)
        if not last:
            keys()
            hold(s)
            election(s)

    op("S", lambda: Y.dma_start(T.yb[:], T.bb[:]).then_inc(T.sem.o_b, 16), ["bb"], ["yb"], ("o_b", 16))
    emit(plan, g, T)
    Y.wait_ge(T.sem.o_c, 16)
    Y.wait_ge(T.sem.o_b, 16)
    g.wait_ge(T.sem.sent, RO * (len(topo.engines(core, T.cores[(rank + 1) % n])) + len(topo.engines(core, T.cores[(rank - 1) % n]))))
